import numpy as np
import ml_dtypes


def mxq(x, axis, fmt="e4m3"):
    dtype, down = {"e4m3": (ml_dtypes.float8_e4m3fn, 7), "e5m2": (ml_dtypes.float8_e5m2, 14)}[fmt]
    v = np.moveaxis(np.asarray(x, np.float32).astype(ml_dtypes.bfloat16).astype(np.float64), axis, -1)
    blocks = v.reshape(v.shape[:-1] + (-1, 32))
    amax = np.abs(blocks).max(-1, keepdims=True)
    byte = np.maximum(np.where(amax > 0, np.frexp(amax)[1] - 1 + 127, 0) - down, 1)
    scale = np.exp2(byte - 127.0)
    codes = (blocks / scale).astype(np.float32).astype(dtype).astype(np.float64)
    return np.moveaxis((codes * scale).reshape(v.shape), -1, axis)


WIDE = False


def mx_kscale(k):
    if not WIDE:
        return np.ones(k)
    levels = np.array([30, -30])
    if k % 512:
        return np.exp2(np.random.permutation(np.resize(levels, k // 32))).repeat(32)
    a = np.empty((k // 512, 16))
    for p in range(k // 512):
        a[p, :8] = np.random.permutation(np.resize(levels, 8))
        for g in range(8):
            far = levels[np.abs(levels - a[p, g]) >= 10]
            a[p, g + 8] = far[np.random.randint(len(far))]
    return np.exp2(a.ravel()).repeat(32)


BF16 = ml_dtypes.bfloat16


def bf(x):
    return np.asarray(x, np.float32).astype(BF16)


def f64(x):
    return np.asarray(x).astype(np.float64)


M, U, V, N = 1024, 2048, 1024, 1536

BETA = 0.6
SIG = 1.25
SIG_HEAVY = 1.5


def setup_inputs():
    s, t = mx_kscale(U), mx_kscale(V)
    iu = np.random.lognormal(-SIG ** 2 / 2, SIG, (M, U)) / np.sqrt(U)
    ui = np.random.lognormal(-SIG ** 2 / 2, SIG, (U, N)) / np.sqrt(U)
    iv = np.random.lognormal(-SIG_HEAVY ** 2 / 2, SIG_HEAVY, (M, V)) / np.sqrt(V)
    vi = np.random.lognormal(-SIG ** 2 / 2, SIG, (V, N)) / np.sqrt(V)
    return {"iu": bf(iu * s),
            "ui": bf(ui / s[:, None]),
            "iv": bf(iv * t),
            "vi": bf(vi / t[:, None]),
            "pop": bf(0.5 + np.random.lognormal(0.0, 0.5, (N,)))}


def reference(iu, ui, iv, vi, pop):
    regular = mxq(f64(iu), 1, "e4m3") @ mxq(f64(ui), 0, "e4m3")
    heavy = mxq(f64(iv), 1, "e5m2") @ mxq(f64(vi), 0, "e4m3")
    walk = regular + heavy
    penalty = f64(pop) ** BETA
    return walk / penalty[None, :]

@@ -1,0 +1,572 @@
+from contextlib import ExitStack
+
+import concourse.mybir as mybir
+from concourse.masks import make_identity
+
+F32 = mybir.dt.float32
+BF16 = mybir.dt.bfloat16
+U32 = mybir.dt.uint32
+U8 = mybir.dt.uint8
+E4M3X4 = mybir.dt.float8_e4m3fn_x4
+E5M2X4 = mybir.dt.float8_e5m2_x4
+
+M, U, V, N = 1024, 2048, 1024, 1536
+FLOPS = 2 * M * N * (U + V)
+P = 128
+K_PASS = 512
+U_PASSES = U // K_PASS
+V_PASSES = V // K_PASS
+PASSES = U_PASSES + V_PASSES
+M_TILES = M // P
+N_TILE = 512
+N_TILES = N // N_TILE
+BETA = 0.6
+POP_COLS = N // P
+TP = 4
+
+
+def tile_rp3beta_item_walk_s2_kernel(tc, iu, ui, iv, vi, pop, out):
+    nc = tc.nc
+    with ExitStack() as ctx:
+        const = ctx.enter_context(tc.tile_pool(name="const", bufs=1))
+        araw_pool = ctx.enter_context(tc.tile_pool(name="araw", bufs=8))
+        agrp_pool = ctx.enter_context(tc.tile_pool(name="agrp", bufs=3))
+        aperm_pool = ctx.enter_context(tc.tile_pool(name="aperm", bufs=2))
+        codes_pool = ctx.enter_context(tc.tile_pool(name="codes", bufs=1))
+        braw_pool = ctx.enter_context(tc.tile_pool(name="braw", bufs=10))
+        bgrp_pool = ctx.enter_context(tc.tile_pool(name="bgrp", bufs=4))
+        res_pool = ctx.enter_context(tc.tile_pool(name="res", bufs=6))
+        acc_pool = ctx.enter_context(tc.psum_pool(name="acc", bufs=4))
+
+        pop_sb = const.tile([P, POP_COLS], BF16, name="pop_sb")
+        nc.scalar.dma_start(out=pop_sb[:], in_=pop.rearrange("(p c) -> p c", c=POP_COLS))
+        ident = const.tile([P, P], F32, name="ident")
+        make_identity(nc, ident[:])
+        power = const.tile([P, POP_COLS], F32, name="power")
+        nc.gpsimd.memset(power[:], 1.0)
+        nc.gpsimd.tensor_scalar(power[:], power[:], -BETA, None, op0=mybir.AluOpType.mult)
+        w_col = const.tile([P, POP_COLS], F32, name="w_col")
+        nc.gpsimd.tensor_tensor(w_col[:], pop_sb[:], power[:], op=mybir.AluOpType.pow)
+        w_row = const.tile([P, N], F32, name="w_row")
+
+        a_raw = {}
+        b_raw = {}
+        a_codes = {}
+        a_perm = {}
+        accs = {}
+        res = {}
+        a_grp = {}
+        b_grp = {}
+        banks = {}
+        a_scales = {}
+        b_codes = {}
+        b_scales = {}
+
+        def load_a(m, pieces):
+            raw = araw_pool.tile([P, U + V], BF16, name="a_raw")
+            rows = slice(m * P, (m + 1) * P)
+            step = U // pieces
+            for c in range(0, U, step):
+                nc.sync.dma_start(out=raw[:, c : c + step], in_=iu[rows, c : c + step])
+            nc.sync.dma_start(out=raw[:, U:], in_=iv[rows, :])
+            a_raw[m] = raw
+
+        def load_b(g, n):
+            raw = braw_pool.tile([P, 4, N_TILE], BF16, name="b_raw")
+            src, row = (ui, g) if g < U_PASSES else (vi, g - U_PASSES)
+            cols = slice(n * N_TILE, (n + 1) * N_TILE)
+            nc.sync.dma_start(
+                out=raw[:],
+                in_=src[row * K_PASS : (row + 1) * K_PASS, cols].rearrange("(p j) w -> p j w", j=4),
+            )
+            b_raw[g, n] = raw
+
+        def permute_a(m, engine_copy):
+            words = a_raw[m][:].bitcast(F32)
+            perm = aperm_pool.tile([P, PASSES, 2, P], F32, name="a_perm", align_bytes=64)
+            engine_copy(out=perm[:], in_=words.rearrange("p (g w u) -> p g u w", u=2, w=P))
+            a_perm[m] = perm
+
+        w_view = w_row[:].rearrange("p (n c) -> p n c", c=POP_COLS)
+
+        def spread_pop(q, pool):
+            banks["w", q] = pool.tile([P, 4, P], F32, name="tp")
+            for c in range(4):
+                col = 4 * q + c
+                nc.tensor.transpose(banks["w", q][:, c, :], w_col[:, col : col + 1].to_broadcast([P, P]), ident[:])
+
+        def gather_pop(q):
+            nc.vector.tensor_copy(out=w_view[:, :, 4 * q : 4 * q + 4], in_=banks["w", q][:].rearrange("p c n -> p n c"))
+
+        def turn_a(m, q, pool):
+            bank = pool.tile([P, 2, 2, P], F32, name="tp")
+            words = a_raw[m][:].bitcast(F32)
+            for h in range(2):
+                g = 2 * q + h
+                for u in range(2):
+                    if m in a_perm:
+                        piece = a_perm[m][:, g, u, :]
+                    else:
+                        piece = words[:, 256 * g + u : 256 * (g + 1) : 2]
+                    nc.tensor.transpose(bank[:, h, u, :], piece, ident[:])
+            banks[m, q] = bank
+
+        def evac_a(m, q, engine_copy):
+            if q == 0:
+                a_grp[m] = agrp_pool.tile([P, PASSES, P, 4], BF16, name="a_grp", align_bytes=64)
+            engine_copy(
+                out=a_grp[m][:, 2 * q : 2 * q + 2].rearrange("p g r t -> p g (r t)").bitcast(F32).rearrange("p g (r u) -> p g r u", u=2),
+                in_=banks[m, q][:].rearrange("p g u r -> p g r u"),
+            )
+
+        def quant_a(m, part):
+            if part == 0:
+                a_codes[m] = codes_pool.tile([P, PASSES * P], U32, name="a_codes%d" % m, align_bytes=64)
+                a_scales[m] = codes_pool.tile([P, PASSES * P], U8, name="a_scales%d" % m, align_bytes=64)
+            flat = a_grp[m][:].rearrange("p g r t -> p (g r t)")
+            split = U_PASSES * P
+            cols = slice(0, split) if part == 0 else slice(split, PASSES * P)
+            fmt = E4M3X4 if part == 0 else E5M2X4
+            nc.vector.quantize_mx(
+                out=a_codes[m][:, cols].bitcast(fmt),
+                scales=a_scales[m][:, cols],
+                in_=flat[:, 4 * cols.start : 4 * cols.stop],
+            )
+
+        def mix_b(g, n, x, on_vector):
+            if (g, n) not in b_grp:
+                b_grp[g, n] = bgrp_pool.tile([P, N_TILE, 4], BF16, name="b_grp", align_bytes=64)
+            src = b_raw[g, n][:].rearrange("p t (c i) -> p c t i", i=4)
+            dst = b_grp[g, n][:].rearrange("p (c i) t -> p c t i", i=4)
+            if on_vector:
+                nc.vector.tensor_copy(out=dst[:, : x // 4], in_=src[:, : x // 4])
+            else:
+                nc.scalar.copy(out=dst[:, x // 4 :], in_=src[:, x // 4 :])
+
+        def quant_b(g, n):
+            b_codes[g, n] = codes_pool.tile([P, N_TILE], U32, name="b_codes%d_%d" % (g, n), align_bytes=64)
+            b_scales[g, n] = codes_pool.tile([P, N_TILE], U8, name="b_scales%d_%d" % (g, n), align_bytes=64)
+            nc.vector.quantize_mx(
+                out=b_codes[g, n][:].bitcast(E4M3X4),
+                scales=b_scales[g, n][:],
+                in_=b_grp[g, n][:].rearrange("p w t -> p (w t)"),
+            )
+
+        def multiply(m, g, n, pool):
+            if g == 0:
+                accs[m, n] = pool.tile([P, N_TILE], F32, name="acc")
+            fmt = E4M3X4 if g < U_PASSES else E5M2X4
+            cols = slice(g * P, (g + 1) * P)
+            nc.tensor.matmul_mx(
+                out=accs[m, n][:],
+                lhsT=a_codes[m][:, cols].bitcast(fmt),
+                lhsT_scale=a_scales[m][:, cols],
+                rhs=b_codes[g, n][:].bitcast(E4M3X4),
+                rhs_scale=b_scales[g, n][:],
+                start=(g == 0),
+                stop=(g == PASSES - 1),
+            )
+
+        def scale(m, n, h, parts):
+            if h == 0:
+                res[m, n] = res_pool.tile([P, N_TILE], F32, name="res_tile")
+            w = N_TILE // parts
+            nc.vector.tensor_tensor(
+                res[m, n][:, h * w : (h + 1) * w],
+                accs[m, n][:, h * w : (h + 1) * w],
+                w_row[:, n * N_TILE + h * w : n * N_TILE + (h + 1) * w],
+                op=mybir.AluOpType.mult,
+            )
+
+        def store(m, n, h, parts):
+            w = N_TILE // parts
+            nc.sync.dma_start(
+                out=out[m * P : (m + 1) * P, n * N_TILE + h * w : n * N_TILE + (h + 1) * w],
+                in_=res[m, n][:, h * w : (h + 1) * w],
+            )
+
+
+        tp = [None]
+
+        def run(name, a):
+            if name == "la":
+                load_a(a[0], a[1])
+            elif name == "lb":
+                load_b(a[0], a[1])
+            elif name == "pw":
+                spread_pop(a[0], tp[0])
+            elif name == "gw":
+                gather_pop(a[0])
+            elif name == "pa":
+                permute_a(a[0], nc.vector.tensor_copy)
+            elif name == "tu":
+                turn_a(a[0], a[1], tp[0])
+            elif name == "ev":
+                evac_a(a[0], a[1], nc.scalar.copy if a[2] == 0 else nc.vector.tensor_copy)
+            elif name == "qa":
+                quant_a(a[0], a[1])
+            elif name == "mv":
+                mix_b(a[0], a[1], a[2], True)
+            elif name == "ms":
+                mix_b(a[0], a[1], a[2], False)
+            elif name == "qb":
+                quant_b(a[0], a[1])
+            elif name == "mm":
+                multiply(a[0], a[1], a[2], acc_pool if a[3] == 0 else acc2_pool)
+            elif name == "sc":
+                scale(a[0], a[1], a[2], a[3])
+            elif name == "st":
+                store(a[0], a[1], a[2], a[3])
+
+        part1, part2 = ([("la", (0, 2,)),
+("la", (1, 1,)),
+("tu", (0, 0,)),
+("tu", (0, 1,)),
+("ev", (0, 0, 0,)),
+("tu", (0, 2,)),
+("la", (2, 1,)),
+("ev", (0, 1, 0,)),
+("pw", (0,)),
+("ev", (0, 2, 0,)),
+("qa", (0, 0,)),
+("pw", (1,)),
+("pw", (2,)),
+("gw", (0,)),
+("tu", (1, 0,)),
+("la", (3, 1,)),
+("qa", (0, 1,)),
+("tu", (1, 1,)),
+("gw", (1,)),
+("ev", (1, 0, 0,)),
+("gw", (2,)),
+("ev", (1, 1, 0,)),
+("tu", (1, 2,)),
+("tu", (2, 0,)),
+("qa", (1, 0,)),
+("lb", (0, 0,)),
+("ev", (1, 2, 0,)),
+("tu", (2, 1,)),
+("ev", (2, 0, 0,)),
+("qa", (1, 1,)),
+("tu", (2, 2,)),
+("ev", (2, 1, 0,)),
+("tu", (3, 0,)),
+("lb", (1, 0,)),
+("ev", (2, 2, 0,)),
+("qa", (2, 0,)),
+("tu", (3, 1,)),
+("ev", (3, 0, 0,)),
+("qa", (2, 1,)),
+("tu", (3, 2,)),
+("ev", (3, 1, 0,)),
+("la", (4, 1,)),
+("mv", (0, 0, 256,)),
+("ev", (3, 2, 0,)),
+("ms", (0, 0, 256,)),
+("qa", (3, 0,)),
+("qa", (3, 1,)),
+("lb", (2, 0,)),
+("mv", (1, 0, 256,)),
+("ms", (1, 0, 256,)),
+("qb", (0, 0,)),
+("tu", (4, 0,)),
+("lb", (3, 0,)),
+("mm", (0, 0, 0, 0,)),
+("qb", (1, 0,)),
+("mm", (1, 0, 0, 0,)),
+("mm", (2, 0, 0, 0,)),
+("mm", (3, 0, 0, 0,)),
+("mm", (0, 1, 0, 0,)),
+("la", (5, 1,)),
+("mm", (1, 1, 0, 0,)),
+("mv", (2, 0, 256,)),
+("ms", (2, 0, 256,)),
+("mm", (2, 1, 0, 0,)),
+("mm", (3, 1, 0, 0,)),
+("tu", (4, 1,)),
+("ev", (4, 0, 0,)),
+("qb", (2, 0,)),
+("lb", (4, 0,)),
+("tu", (4, 2,)),
+("ms", (3, 0, 256,)),
+("mv", (3, 0, 256,)),
+("mm", (0, 2, 0, 0,)),
+("mm", (1, 2, 0, 0,)),
+("mm", (2, 2, 0, 0,)),
+("lb", (5, 0,)),
+("mm", (3, 2, 0, 0,)),
+("ev", (4, 1, 0,)),
+("qb", (3, 0,)),
+("tu", (5, 0,)),
+("ev", (4, 2, 0,)),
+("qa", (4, 0,)),
+("mm", (0, 3, 0, 0,)),
+("ev", (5, 0, 0,)),
+("la", (6, 1,)),
+("qa", (4, 1,)),
+("mm", (1, 3, 0, 0,)),
+("mm", (2, 3, 0, 0,)),
+("mv", (4, 0, 256,)),
+("ms", (4, 0, 256,)),
+("mm", (3, 3, 0, 0,)),
+("tu", (5, 1,)),
+("tu", (5, 2,)),
+("ev", (5, 1, 0,)),
+("qb", (4, 0,)),
+("la", (7, 1,)),
+("ms", (5, 0, 256,)),
+("mv", (5, 0, 256,)),
+("mm", (0, 4, 0, 0,)),
+("mm", (1, 4, 0, 0,)),
+("qa", (5, 0,)),
+("mm", (2, 4, 0, 0,)),
+("mm", (3, 4, 0, 0,)),
+("ev", (5, 2, 0,)),
+("lb", (0, 1,)),
+("qb", (5, 0,)),
+("tu", (6, 0,)),
+("qa", (5, 1,)),
+("tu", (6, 1,)),
+("ev", (6, 0, 0,)),
+("mm", (0, 5, 0, 0,)),
+("mm", (1, 5, 0, 0,)),
+("sc", (0, 0, 0, 1,)),
+("mm", (2, 5, 0, 0,)),
+("lb", (1, 1,)),
+("mm", (3, 5, 0, 0,)),
+("sc", (1, 0, 0, 1,)),
+("mm", (4, 0, 0, 0,)),
+("sc", (2, 0, 0, 1,)),
+("mm", (4, 1, 0, 0,)),
+("lb", (2, 1,)),
+("mm", (4, 2, 0, 0,)),
+("sc", (3, 0, 0, 1,)),
+("mm", (4, 3, 0, 0,)),
+("ms", (0, 1, 208,)),
+("mm", (4, 4, 0, 0,)),
+("mv", (0, 1, 208,)),
+("mm", (4, 5, 0, 0,)),
+("mm", (5, 0, 0, 0,)),
+("sc", (4, 0, 0, 1,)),
+("lb", (3, 1,)),
+("mm", (5, 1, 0, 0,)),
+("mm", (5, 2, 0, 0,)),
+("ms", (1, 1, 208,)),
+("qb", (0, 1,)),
+("mm", (5, 3, 0, 0,)),
+("mm", (5, 4, 0, 0,)),
+("mv", (1, 1, 208,)),
+("mm", (5, 5, 0, 0,)),
+("lb", (4, 1,)),
+("sc", (5, 0, 0, 1,)),
+("tu", (6, 2,)),
+("ms", (2, 1, 208,)),
+("qb", (1, 1,)),
+("tu", (7, 0,)),
+("mv", (2, 1, 208,)),
+("lb", (5, 1,)),
+("tu", (7, 1,)),
+("ev", (6, 1, 0,)),
+("mv", (3, 1, 208,)),
+("ev", (6, 2, 0,)),
+("qb", (2, 1,)),
+("tu", (7, 2,)),
+("lb", (0, 2,)),
+("ev", (7, 0, 0,)),
+("qa", (6, 0,)),
+("ev", (7, 1, 0,)),
+("qa", (6, 1,)),
+("mm", (6, 0, 0, 0,)),
+("mv", (4, 1, 208,)),
+("ev", (7, 2, 0,))],
+[("mm", (4, 0, 1, 1,)),
+("mm", (6, 1, 0, 0,)),
+("lb", (1, 2,)),
+("mm", (6, 2, 0, 0,)),
+("qa", (7, 0,)),
+("ms", (3, 1, 208,)),
+("mm", (6, 3, 0, 0,)),
+("mm", (6, 4, 0, 0,)),
+("qa", (7, 1,)),
+("mm", (6, 5, 0, 0,)),
+("mv", (5, 1, 208,)),
+("mm", (7, 0, 0, 0,)),
+("lb", (2, 2,)),
+("mm", (7, 1, 0, 0,)),
+("mv", (0, 2, 208,)),
+("ms", (4, 1, 208,)),
+("mm", (7, 2, 0, 0,)),
+("mm", (7, 3, 0, 0,)),
+("qb", (3, 1,)),
+("mm", (7, 4, 0, 0,)),
+("mm", (7, 5, 0, 0,)),
+("st", (0, 0, 0, 1,)),
+("mm", (0, 0, 1, 0,)),
+("mv", (1, 2, 208,)),
+("mm", (1, 0, 1, 0,)),
+("ms", (5, 1, 208,)),
+("st", (1, 0, 0, 1,)),
+("mm", (5, 0, 1, 1,)),
+("qb", (4, 1,)),
+("mm", (6, 0, 1, 1,)),
+("st", (2, 0, 0, 1,)),
+("mm", (7, 0, 1, 1,)),
+("mm", (0, 1, 1, 0,)),
+("mv", (2, 2, 208,)),
+("mm", (1, 1, 1, 0,)),
+("st", (3, 0, 0, 1,)),
+("ms", (0, 2, 208,)),
+("mm", (4, 1, 1, 1,)),
+("qb", (5, 1,)),
+("mm", (5, 1, 1, 1,)),
+("st", (4, 0, 0, 1,)),
+("mm", (6, 1, 1, 1,)),
+("sc", (6, 0, 0, 1,)),
+("mm", (7, 1, 1, 1,)),
+("st", (5, 0, 0, 1,)),
+("mm", (0, 2, 1, 0,)),
+("ms", (1, 2, 208,)),
+("sc", (7, 0, 0, 1,)),
+("mm", (1, 2, 1, 0,)),
+("lb", (3, 2,)),
+("mm", (2, 0, 1, 0,)),
+("qb", (0, 2,)),
+("mm", (2, 1, 1, 0,)),
+("mm", (3, 0, 1, 0,)),
+("mm", (3, 1, 1, 0,)),
+("ms", (2, 2, 208,)),
+("mm", (2, 2, 1, 0,)),
+("qb", (1, 2,)),
+("mm", (3, 2, 1, 0,)),
+("lb", (4, 2,)),
+("mm", (4, 2, 1, 1,)),
+("mm", (5, 2, 1, 1,)),
+("mm", (6, 2, 1, 1,)),
+("mm", (7, 2, 1, 1,)),
+("qb", (2, 2,)),
+("mm", (0, 3, 1, 0,)),
+("lb", (5, 2,)),
+("mm", (0, 4, 1, 0,)),
+("ms", (3, 2, 208,)),
+("mv", (3, 2, 208,)),
+("mm", (0, 5, 1, 0,)),
+("mm", (1, 3, 1, 0,)),
+("sc", (0, 1, 0, 1,)),
+("mm", (1, 4, 1, 0,)),
+("mm", (1, 5, 1, 0,)),
+("st", (6, 0, 0, 1,)),
+("mm", (2, 3, 1, 0,)),
+("mv", (4, 2, 208,)),
+("ms", (4, 2, 208,)),
+("mm", (2, 4, 1, 0,)),
+("st", (7, 0, 0, 1,)),
+("mm", (2, 5, 1, 0,)),
+("sc", (1, 1, 0, 1,)),
+("mm", (3, 3, 1, 0,)),
+("st", (0, 1, 0, 1,)),
+("mm", (3, 4, 1, 0,)),
+("sc", (2, 1, 0, 1,)),
+("mm", (3, 5, 1, 0,)),
+("ms", (5, 2, 208,)),
+("st", (1, 1, 0, 1,)),
+("mm", (4, 3, 1, 1,)),
+("qb", (3, 2,)),
+("mm", (4, 4, 1, 1,)),
+("mm", (4, 5, 1, 1,)),
+("st", (2, 1, 0, 1,)),
+("sc", (3, 1, 0, 1,)),
+("mm", (5, 3, 1, 1,)),
+("mm", (5, 4, 1, 1,)),
+("sc", (4, 1, 0, 1,)),
+("mm", (5, 5, 1, 1,)),
+("st", (3, 1, 0, 1,)),
+("mm", (6, 3, 1, 1,)),
+("qb", (4, 2,)),
+("mm", (6, 4, 1, 1,)),
+("st", (4, 1, 0, 1,)),
+("mm", (6, 5, 1, 1,)),
+("sc", (5, 1, 0, 1,)),
+("mm", (7, 3, 1, 1,)),
+("mm", (7, 4, 1, 1,)),
+("sc", (6, 1, 0, 1,)),
+("mm", (7, 5, 1, 1,)),
+("st", (5, 1, 0, 1,)),
+("mm", (0, 0, 2, 0,)),
+("mv", (5, 2, 208,)),
+("mm", (1, 0, 2, 0,)),
+("st", (6, 1, 0, 1,)),
+("mm", (2, 0, 2, 0,)),
+("sc", (7, 1, 0, 1,)),
+("mm", (3, 0, 2, 0,)),
+("mm", (4, 0, 2, 1,)),
+("qb", (5, 2,)),
+("mm", (5, 0, 2, 1,)),
+("st", (7, 1, 0, 1,)),
+("mm", (6, 0, 2, 1,)),
+("mm", (7, 0, 2, 1,)),
+("mm", (0, 1, 2, 0,)),
+("mm", (1, 1, 2, 0,)),
+("mm", (2, 1, 2, 0,)),
+("mm", (3, 1, 2, 0,)),
+("mm", (4, 1, 2, 1,)),
+("mm", (5, 1, 2, 1,)),
+("mm", (6, 1, 2, 1,)),
+("mm", (7, 1, 2, 1,)),
+("mm", (0, 2, 2, 0,)),
+("mm", (1, 2, 2, 0,)),
+("mm", (2, 2, 2, 0,)),
+("mm", (3, 2, 2, 0,)),
+("mm", (4, 2, 2, 1,)),
+("mm", (5, 2, 2, 1,)),
+("mm", (6, 2, 2, 1,)),
+("mm", (7, 2, 2, 1,)),
+("mm", (0, 3, 2, 0,)),
+("mm", (0, 4, 2, 0,)),
+("mm", (0, 5, 2, 0,)),
+("mm", (1, 3, 2, 0,)),
+("sc", (0, 2, 0, 1,)),
+("mm", (1, 4, 2, 0,)),
+("mm", (1, 5, 2, 0,)),
+("mm", (2, 3, 2, 0,)),
+("st", (0, 2, 0, 1,)),
+("sc", (1, 2, 0, 1,)),
+("mm", (2, 4, 2, 0,)),
+("mm", (2, 5, 2, 0,)),
+("mm", (3, 3, 2, 0,)),
+("st", (1, 2, 0, 1,)),
+("sc", (2, 2, 0, 1,)),
+("mm", (3, 4, 2, 0,)),
+("mm", (3, 5, 2, 0,)),
+("mm", (4, 3, 2, 1,)),
+("st", (2, 2, 0, 1,)),
+("sc", (3, 2, 0, 1,)),
+("mm", (4, 4, 2, 1,)),
+("mm", (4, 5, 2, 1,)),
+("mm", (5, 3, 2, 1,)),
+("st", (3, 2, 0, 1,)),
+("sc", (4, 2, 0, 1,)),
+("mm", (5, 4, 2, 1,)),
+("mm", (5, 5, 2, 1,)),
+("mm", (6, 3, 2, 1,)),
+("st", (4, 2, 0, 1,)),
+("sc", (5, 2, 0, 1,)),
+("mm", (6, 4, 2, 1,)),
+("mm", (6, 5, 2, 1,)),
+("mm", (7, 3, 2, 1,)),
+("st", (5, 2, 0, 1,)),
+("sc", (6, 2, 0, 1,)),
+("mm", (7, 4, 2, 1,)),
+("mm", (7, 5, 2, 1,)),
+("st", (6, 2, 0, 1,)),
+("sc", (7, 2, 0, 2,)),
+("sc", (7, 2, 1, 2,)),
+("st", (7, 2, 0, 2,)),
+("st", (7, 2, 1, 2,))])
+        with tc.manual_schedule():
+            with tc.psum_pool(name="tp", bufs=TP) as tp_pool:
+                tp[0] = tp_pool
+                for name, a in part1:
+                    run(name, a)
+            acc2_pool = ctx.enter_context(tc.psum_pool(name="acc2", bufs=TP))
+            for name, a in part2:
+                run(name, a)

@@ -31,7 +31,7 @@ def tile_rp3beta_item_walk_s2_kernel(tc, iu, ui, iv, vi, pop, out):
         const = ctx.enter_context(tc.tile_pool(name="const", bufs=1))
         araw_pool = ctx.enter_context(tc.tile_pool(name="araw", bufs=8))
         agrp_pool = ctx.enter_context(tc.tile_pool(name="agrp", bufs=3))
-        aperm_pool = ctx.enter_context(tc.tile_pool(name="aperm", bufs=2))
+        aperm_pool = ctx.enter_context(tc.tile_pool(name="aperm", bufs=4))
         codes_pool = ctx.enter_context(tc.tile_pool(name="codes", bufs=1))
         braw_pool = ctx.enter_context(tc.tile_pool(name="braw", bufs=10))
         bgrp_pool = ctx.enter_context(tc.tile_pool(name="bgrp", bufs=4))
@@ -81,11 +81,10 @@ def tile_rp3beta_item_walk_s2_kernel(tc, iu, ui, iv, vi, pop, out):
             )
             b_raw[g, n] = raw
 
-        def permute_a(m, engine_copy):
-            words = a_raw[m][:].bitcast(F32)
-            perm = aperm_pool.tile([P, PASSES, 2, P], F32, name="a_perm", align_bytes=64)
-            engine_copy(out=perm[:], in_=words.rearrange("p (g w u) -> p g u w", u=2, w=P))
-            a_perm[m] = perm
+        def permute_a(m, q):
+            words = a_raw[m][:, 1024 * q : 1024 * (q + 1)].bitcast(F32)
+            a_perm[m, q] = aperm_pool.tile([P, 2, 2, P], F32, name="a_perm", align_bytes=64)
+            nc.vector.tensor_copy(out=a_perm[m, q][:], in_=words.rearrange("p (g w u) -> p g u w", u=2, w=P))
 
         w_view = w_row[:].rearrange("p (n c) -> p n c", c=POP_COLS)
 
@@ -104,15 +103,15 @@ def tile_rp3beta_item_walk_s2_kernel(tc, iu, ui, iv, vi, pop, out):
             for h in range(2):
                 g = 2 * q + h
                 for u in range(2):
-                    if m in a_perm:
-                        piece = a_perm[m][:, g, u, :]
+                    if (m, q) in a_perm:
+                        piece = a_perm[m, q][:, h, u, :]
                     else:
                         piece = words[:, 256 * g + u : 256 * (g + 1) : 2]
                     nc.tensor.transpose(bank[:, h, u, :], piece, ident[:])
             banks[m, q] = bank
 
         def evac_a(m, q, engine_copy):
-            if q == 0:
+            if m not in a_grp:
                 a_grp[m] = agrp_pool.tile([P, PASSES, P, 4], BF16, name="a_grp", align_bytes=64)
             engine_copy(
                 out=a_grp[m][:, 2 * q : 2 * q + 2].rearrange("p g r t -> p g (r t)").bitcast(F32).rearrange("p g (r u) -> p g r u", u=2),
@@ -120,7 +119,7 @@ def tile_rp3beta_item_walk_s2_kernel(tc, iu, ui, iv, vi, pop, out):
             )
 
         def quant_a(m, part):
-            if part == 0:
+            if m not in a_codes:
                 a_codes[m] = codes_pool.tile([P, PASSES * P], U32, name="a_codes%d" % m, align_bytes=64)
                 a_scales[m] = codes_pool.tile([P, PASSES * P], U8, name="a_scales%d" % m, align_bytes=64)
             flat = a_grp[m][:].rearrange("p g r t -> p (g r t)")
@@ -168,7 +167,7 @@ def tile_rp3beta_item_walk_s2_kernel(tc, iu, ui, iv, vi, pop, out):
             )
 
         def scale(m, n, h, parts):
-            if h == 0:
+            if (m, n) not in res:
                 res[m, n] = res_pool.tile([P, N_TILE], F32, name="res_tile")
             w = N_TILE // parts
             nc.vector.tensor_tensor(
@@ -198,7 +197,7 @@ def tile_rp3beta_item_walk_s2_kernel(tc, iu, ui, iv, vi, pop, out):
             elif name == "gw":
                 gather_pop(a[0])
             elif name == "pa":
-                permute_a(a[0], nc.vector.tensor_copy)
+                permute_a(a[0], a[1])
             elif name == "tu":
                 turn_a(a[0], a[1], tp[0])
             elif name == "ev":
@@ -218,350 +217,374 @@ def tile_rp3beta_item_walk_s2_kernel(tc, iu, ui, iv, vi, pop, out):
             elif name == "st":
                 store(a[0], a[1], a[2], a[3])
 
-        part1, part2 = ([("la", (0, 2,)),
+        part1, part2 = ([("lb", (0, 0,)),
+("la", (0, 2,)),
 ("la", (1, 1,)),
-("tu", (0, 0,)),
-("tu", (0, 1,)),
-("ev", (0, 0, 0,)),
-("tu", (0, 2,)),
+("lb", (1, 0,)),
 ("la", (2, 1,)),
-("ev", (0, 1, 0,)),
-("pw", (0,)),
-("ev", (0, 2, 0,)),
-("qa", (0, 0,)),
-("pw", (1,)),
-("pw", (2,)),
-("gw", (0,)),
-("tu", (1, 0,)),
+("ms", (0, 0, 256,)),
 ("la", (3, 1,)),
-("qa", (0, 1,)),
-("tu", (1, 1,)),
-("gw", (1,)),
+("pa", (0, 0,)),
+("mv", (0, 0, 256,)),
+("tu", (0, 0,)),
+("pa", (0, 1,)),
+("lb", (2, 0,)),
+("ev", (0, 0, 0,)),
+("pa", (0, 2,)),
+("tu", (0, 1,)),
+("tu", (0, 2,)),
+("ev", (0, 1, 0,)),
+("lb", (3, 0,)),
+("pa", (1, 0,)),
+("qb", (0, 0,)),
+("ev", (0, 2, 0,)),
+("tu", (1, 0,)),
+("lb", (4, 0,)),
+("pa", (1, 1,)),
+("qa", (0, 0,)),
 ("ev", (1, 0, 0,)),
-("gw", (2,)),
-("ev", (1, 1, 0,)),
+("tu", (1, 1,)),
+("pa", (1, 2,)),
+("la", (4, 1,)),
+("qa", (0, 1,)),
+("ms", (1, 0, 256,)),
 ("tu", (1, 2,)),
-("tu", (2, 0,)),
-("qa", (1, 0,)),
-("lb", (0, 0,)),
+("mv", (1, 0, 256,)),
+("pa", (2, 0,)),
 ("ev", (1, 2, 0,)),
+("pa", (2, 1,)),
+("tu", (2, 0,)),
+("lb", (5, 0,)),
+("qb", (1, 0,)),
+("ev", (1, 1, 0,)),
 ("tu", (2, 1,)),
+("pa", (2, 2,)),
 ("ev", (2, 0, 0,)),
 ("qa", (1, 1,)),
 ("tu", (2, 2,)),
+("la", (5, 1,)),
 ("ev", (2, 1, 0,)),
+("pa", (3, 0,)),
+("pa", (3, 1,)),
 ("tu", (3, 0,)),
-("lb", (1, 0,)),
+("qa", (1, 0,)),
 ("ev", (2, 2, 0,)),
-("qa", (2, 0,)),
 ("tu", (3, 1,)),
+("pa", (3, 2,)),
 ("ev", (3, 0, 0,)),
 ("qa", (2, 1,)),
-("tu", (3, 2,)),
-("ev", (3, 1, 0,)),
-("la", (4, 1,)),
-("mv", (0, 0, 256,)),
-("ev", (3, 2, 0,)),
-("ms", (0, 0, 256,)),
-("qa", (3, 0,)),
-("qa", (3, 1,)),
-("lb", (2, 0,)),
-("mv", (1, 0, 256,)),
-("ms", (1, 0, 256,)),
-("qb", (0, 0,)),
-("tu", (4, 0,)),
-("lb", (3, 0,)),
 ("mm", (0, 0, 0, 0,)),
-("qb", (1, 0,)),
+("qa", (2, 0,)),
+("ev", (3, 1, 0,)),
+("lb", (1, 1,)),
 ("mm", (1, 0, 0, 0,)),
-("mm", (2, 0, 0, 0,)),
-("mm", (3, 0, 0, 0,)),
-("mm", (0, 1, 0, 0,)),
-("la", (5, 1,)),
-("mm", (1, 1, 0, 0,)),
 ("mv", (2, 0, 256,)),
 ("ms", (2, 0, 256,)),
-("mm", (2, 1, 0, 0,)),
-("mm", (3, 1, 0, 0,)),
-("tu", (4, 1,)),
-("ev", (4, 0, 0,)),
-("qb", (2, 0,)),
-("lb", (4, 0,)),
-("tu", (4, 2,)),
+("mm", (0, 1, 0, 0,)),
+("qa", (3, 0,)),
+("mm", (1, 1, 0, 0,)),
+("la", (6, 1,)),
 ("ms", (3, 0, 256,)),
 ("mv", (3, 0, 256,)),
-("mm", (0, 2, 0, 0,)),
-("mm", (1, 2, 0, 0,)),
-("mm", (2, 2, 0, 0,)),
-("lb", (5, 0,)),
-("mm", (3, 2, 0, 0,)),
-("ev", (4, 1, 0,)),
-("qb", (3, 0,)),
-("tu", (5, 0,)),
-("ev", (4, 2, 0,)),
-("qa", (4, 0,)),
-("mm", (0, 3, 0, 0,)),
-("ev", (5, 0, 0,)),
-("la", (6, 1,)),
-("qa", (4, 1,)),
-("mm", (1, 3, 0, 0,)),
-("mm", (2, 3, 0, 0,)),
+("tu", (3, 2,)),
+("pw", (0,)),
+("qb", (2, 0,)),
+("pw", (1,)),
+("pw", (2,)),
 ("mv", (4, 0, 256,)),
 ("ms", (4, 0, 256,)),
-("mm", (3, 3, 0, 0,)),
-("tu", (5, 1,)),
-("tu", (5, 2,)),
-("ev", (5, 1, 0,)),
-("qb", (4, 0,)),
+("mm", (2, 0, 0, 0,)),
+("mm", (3, 0, 0, 0,)),
+("qb", (3, 0,)),
+("mm", (1, 2, 0, 0,)),
+("lb", (0, 1,)),
+("mm", (3, 1, 0, 0,)),
+("ev", (3, 2, 0,)),
+("pa", (4, 0,)),
+("mm", (0, 2, 0, 0,)),
+("gw", (0,)),
+("mm", (1, 3, 0, 0,)),
 ("la", (7, 1,)),
+("mm", (2, 1, 0, 0,)),
+("pa", (4, 1,)),
+("mm", (2, 2, 0, 0,)),
+("pa", (4, 2,)),
+("mm", (2, 3, 0, 0,)),
+("qb", (4, 0,)),
+("mm", (0, 3, 0, 0,)),
+("tu", (4, 0,)),
 ("ms", (5, 0, 256,)),
 ("mv", (5, 0, 256,)),
-("mm", (0, 4, 0, 0,)),
+("tu", (4, 1,)),
+("gw", (1,)),
 ("mm", (1, 4, 0, 0,)),
-("qa", (5, 0,)),
-("mm", (2, 4, 0, 0,)),
-("mm", (3, 4, 0, 0,)),
-("ev", (5, 2, 0,)),
-("lb", (0, 1,)),
+("mm", (0, 4, 0, 0,)),
+("ev", (4, 0, 0,)),
 ("qb", (5, 0,)),
-("tu", (6, 0,)),
-("qa", (5, 1,)),
-("tu", (6, 1,)),
-("ev", (6, 0, 0,)),
+("tu", (4, 2,)),
+("ev", (4, 1, 0,)),
+("mm", (2, 4, 0, 0,)),
+("gw", (2,)),
+("mm", (3, 2, 0, 0,)),
+("ev", (4, 2, 0,)),
 ("mm", (0, 5, 0, 0,)),
+("pa", (5, 0,)),
+("mm", (3, 3, 0, 0,)),
+("pa", (5, 1,)),
 ("mm", (1, 5, 0, 0,)),
-("sc", (0, 0, 0, 1,)),
+("pa", (5, 2,)),
+("ms", (1, 1, 160,)),
 ("mm", (2, 5, 0, 0,)),
-("lb", (1, 1,)),
-("mm", (3, 5, 0, 0,)),
-("sc", (1, 0, 0, 1,)),
-("mm", (4, 0, 0, 0,)),
-("sc", (2, 0, 0, 1,)),
-("mm", (4, 1, 0, 0,)),
+("qa", (4, 0,)),
+("tu", (5, 0,)),
+("sc", (0, 0, 0, 1,)),
+("tu", (5, 1,)),
+("tu", (5, 2,)),
+("pa", (6, 0,)),
+("st", (0, 0, 0, 1,)),
 ("lb", (2, 1,)),
+("mm", (4, 0, 0, 0,)),
+("pa", (6, 1,)),
+("ev", (5, 0, 0,)),
+("mm", (4, 1, 0, 0,)),
+("sc", (1, 0, 0, 1,)),
 ("mm", (4, 2, 0, 0,)),
-("sc", (3, 0, 0, 1,)),
-("mm", (4, 3, 0, 0,)),
-("ms", (0, 1, 208,)),
-("mm", (4, 4, 0, 0,)),
-("mv", (0, 1, 208,)),
-("mm", (4, 5, 0, 0,)),
-("mm", (5, 0, 0, 0,)),
-("sc", (4, 0, 0, 1,)),
+("ev", (5, 1, 0,)),
+("qa", (4, 1,)),
+("st", (1, 0, 0, 1,)),
+("tu", (6, 0,)),
 ("lb", (3, 1,)),
+("lb", (4, 1,)),
+("ev", (5, 2, 0,)),
+("tu", (6, 1,)),
+("qa", (5, 0,)),
+("lb", (1, 2,)),
+("mm", (4, 3, 0, 0,)),
+("qa", (3, 1,)),
+("mm", (4, 4, 0, 0,)),
+("mv", (0, 1, 160,)),
+("mm", (5, 0, 0, 0,)),
+("ev", (6, 0, 0,)),
+("mm", (3, 4, 0, 0,)),
+("mv", (1, 1, 160,)),
+("lb", (5, 1,)),
+("mm", (4, 5, 0, 0,)),
+("ev", (6, 1, 0,)),
+("pa", (6, 2,)),
+("mm", (3, 5, 0, 0,)),
+("pa", (7, 0,)),
 ("mm", (5, 1, 0, 0,)),
+("lb", (0, 2,)),
+("ms", (0, 1, 160,)),
+("pa", (7, 1,)),
+("tu", (6, 2,)),
+("pa", (7, 2,)),
+("lb", (2, 2,)),
+("tu", (7, 0,)),
+("qa", (6, 0,)),
+("tu", (7, 1,)),
+("tu", (7, 2,)),
+("sc", (2, 0, 0, 1,)),
+("ev", (7, 1, 0,)),
 ("mm", (5, 2, 0, 0,)),
-("ms", (1, 1, 208,)),
 ("qb", (0, 1,)),
 ("mm", (5, 3, 0, 0,)),
-("mm", (5, 4, 0, 0,)),
-("mv", (1, 1, 208,)),
-("mm", (5, 5, 0, 0,)),
-("lb", (4, 1,)),
-("sc", (5, 0, 0, 1,)),
-("tu", (6, 2,)),
-("ms", (2, 1, 208,)),
-("qb", (1, 1,)),
-("tu", (7, 0,)),
-("mv", (2, 1, 208,)),
-("lb", (5, 1,)),
-("tu", (7, 1,)),
-("ev", (6, 1, 0,)),
-("mv", (3, 1, 208,)),
-("ev", (6, 2, 0,)),
-("qb", (2, 1,)),
-("tu", (7, 2,)),
-("lb", (0, 2,)),
 ("ev", (7, 0, 0,)),
-("qa", (6, 0,)),
-("ev", (7, 1, 0,)),
-("qa", (6, 1,)),
 ("mm", (6, 0, 0, 0,)),
-("mv", (4, 1, 208,)),
-("ev", (7, 2, 0,))],
-[("mm", (4, 0, 1, 1,)),
+("qa", (5, 1,)),
 ("mm", (6, 1, 0, 0,)),
-("lb", (1, 2,)),
+("ev", (7, 2, 0,)),
+("sc", (3, 0, 0, 1,)),
 ("mm", (6, 2, 0, 0,)),
-("qa", (7, 0,)),
-("ms", (3, 1, 208,)),
 ("mm", (6, 3, 0, 0,)),
-("mm", (6, 4, 0, 0,)),
-("qa", (7, 1,)),
-("mm", (6, 5, 0, 0,)),
-("mv", (5, 1, 208,)),
-("mm", (7, 0, 0, 0,)),
-("lb", (2, 2,)),
-("mm", (7, 1, 0, 0,)),
-("mv", (0, 2, 208,)),
-("ms", (4, 1, 208,)),
-("mm", (7, 2, 0, 0,)),
-("mm", (7, 3, 0, 0,)),
-("qb", (3, 1,)),
-("mm", (7, 4, 0, 0,)),
-("mm", (7, 5, 0, 0,)),
-("st", (0, 0, 0, 1,)),
-("mm", (0, 0, 1, 0,)),
-("mv", (1, 2, 208,)),
-("mm", (1, 0, 1, 0,)),
-("ms", (5, 1, 208,)),
-("st", (1, 0, 0, 1,)),
+("ev", (6, 2, 0,))],
+[("qa", (7, 0,)),
+("mm", (4, 0, 1, 1,)),
 ("mm", (5, 0, 1, 1,)),
-("qb", (4, 1,)),
+("ms", (2, 1, 160,)),
+("mv", (2, 1, 160,)),
+("mm", (5, 4, 0, 0,)),
+("mm", (5, 5, 0, 0,)),
+("qa", (6, 1,)),
 ("mm", (6, 0, 1, 1,)),
-("st", (2, 0, 0, 1,)),
-("mm", (7, 0, 1, 1,)),
-("mm", (0, 1, 1, 0,)),
-("mv", (2, 2, 208,)),
-("mm", (1, 1, 1, 0,)),
-("st", (3, 0, 0, 1,)),
-("ms", (0, 2, 208,)),
-("mm", (4, 1, 1, 1,)),
-("qb", (5, 1,)),
+("sc", (4, 0, 0, 1,)),
+("mm", (7, 0, 0, 0,)),
+("mm", (7, 1, 0, 0,)),
+("qb", (1, 1,)),
+("mm", (6, 4, 0, 0,)),
+("ms", (3, 1, 160,)),
+("mm", (6, 5, 0, 0,)),
+("qb", (2, 1,)),
+("mm", (0, 0, 1, 0,)),
+("mm", (7, 2, 0, 0,)),
+("sc", (5, 0, 0, 1,)),
 ("mm", (5, 1, 1, 1,)),
-("st", (4, 0, 0, 1,)),
-("mm", (6, 1, 1, 1,)),
-("sc", (6, 0, 0, 1,)),
-("mm", (7, 1, 1, 1,)),
+("mm", (7, 0, 1, 1,)),
+("qa", (7, 1,)),
 ("st", (5, 0, 0, 1,)),
+("mm", (7, 3, 0, 0,)),
+("mv", (3, 1, 160,)),
+("ms", (4, 1, 160,)),
+("mm", (6, 1, 1, 1,)),
+("mm", (6, 2, 1, 1,)),
+("mv", (4, 1, 160,)),
+("mm", (4, 1, 1, 1,)),
+("qb", (3, 1,)),
+("mm", (1, 0, 1, 0,)),
+("mm", (0, 1, 1, 0,)),
+("sc", (6, 0, 0, 1,)),
+("mm", (7, 4, 0, 0,)),
+("ms", (1, 2, 160,)),
 ("mm", (0, 2, 1, 0,)),
-("ms", (1, 2, 208,)),
+("qb", (4, 1,)),
+("mm", (4, 2, 1, 1,)),
+("mm", (7, 5, 0, 0,)),
+("mm", (0, 3, 1, 0,)),
 ("sc", (7, 0, 0, 1,)),
-("mm", (1, 2, 1, 0,)),
-("lb", (3, 2,)),
+("mm", (5, 2, 1, 1,)),
+("mm", (5, 3, 1, 1,)),
+("mv", (5, 1, 160,)),
+("ms", (5, 1, 160,)),
 ("mm", (2, 0, 1, 0,)),
-("qb", (0, 2,)),
+("st", (7, 0, 0, 1,)),
+("st", (2, 0, 0, 1,)),
+("st", (3, 0, 0, 1,)),
+("mm", (1, 1, 1, 0,)),
+("lb", (3, 2,)),
+("mv", (0, 2, 160,)),
+("st", (4, 0, 0, 1,)),
+("mm", (0, 4, 1, 0,)),
+("st", (6, 0, 0, 1,)),
+("lb", (4, 2,)),
+("mv", (1, 2, 160,)),
 ("mm", (2, 1, 1, 0,)),
 ("mm", (3, 0, 1, 0,)),
-("mm", (3, 1, 1, 0,)),
-("ms", (2, 2, 208,)),
-("mm", (2, 2, 1, 0,)),
-("qb", (1, 2,)),
-("mm", (3, 2, 1, 0,)),
-("lb", (4, 2,)),
-("mm", (4, 2, 1, 1,)),
-("mm", (5, 2, 1, 1,)),
-("mm", (6, 2, 1, 1,)),
-("mm", (7, 2, 1, 1,)),
-("qb", (2, 2,)),
-("mm", (0, 3, 1, 0,)),
 ("lb", (5, 2,)),
-("mm", (0, 4, 1, 0,)),
-("ms", (3, 2, 208,)),
-("mv", (3, 2, 208,)),
-("mm", (0, 5, 1, 0,)),
-("mm", (1, 3, 1, 0,)),
-("sc", (0, 1, 0, 1,)),
-("mm", (1, 4, 1, 0,)),
-("mm", (1, 5, 1, 0,)),
-("st", (6, 0, 0, 1,)),
+("mm", (2, 2, 1, 0,)),
 ("mm", (2, 3, 1, 0,)),
-("mv", (4, 2, 208,)),
-("ms", (4, 2, 208,)),
-("mm", (2, 4, 1, 0,)),
-("st", (7, 0, 0, 1,)),
-("mm", (2, 5, 1, 0,)),
-("sc", (1, 1, 0, 1,)),
-("mm", (3, 3, 1, 0,)),
-("st", (0, 1, 0, 1,)),
-("mm", (3, 4, 1, 0,)),
-("sc", (2, 1, 0, 1,)),
-("mm", (3, 5, 1, 0,)),
-("ms", (5, 2, 208,)),
-("st", (1, 1, 0, 1,)),
-("mm", (4, 3, 1, 1,)),
-("qb", (3, 2,)),
-("mm", (4, 4, 1, 1,)),
-("mm", (4, 5, 1, 1,)),
-("st", (2, 1, 0, 1,)),
-("sc", (3, 1, 0, 1,)),
-("mm", (5, 3, 1, 1,)),
+("ms", (0, 2, 160,)),
+("qb", (5, 1,)),
+("mm", (1, 2, 1, 0,)),
 ("mm", (5, 4, 1, 1,)),
-("sc", (4, 1, 0, 1,)),
-("mm", (5, 5, 1, 1,)),
-("st", (3, 1, 0, 1,)),
+("mv", (2, 2, 160,)),
+("mm", (1, 3, 1, 0,)),
+("mm", (2, 4, 1, 0,)),
+("mm", (4, 3, 1, 1,)),
+("mm", (3, 1, 1, 0,)),
+("ms", (2, 2, 160,)),
+("mm", (3, 2, 1, 0,)),
+("mm", (3, 3, 1, 0,)),
 ("mm", (6, 3, 1, 1,)),
-("qb", (4, 2,)),
+("mm", (1, 4, 1, 0,)),
+("mm", (0, 5, 1, 0,)),
+("mm", (7, 1, 1, 1,)),
+("ms", (3, 2, 160,)),
+("sc", (0, 1, 0, 1,)),
+("mm", (2, 5, 1, 0,)),
 ("mm", (6, 4, 1, 1,)),
-("st", (4, 1, 0, 1,)),
-("mm", (6, 5, 1, 1,)),
-("sc", (5, 1, 0, 1,)),
+("qb", (1, 2,)),
+("mm", (1, 5, 1, 0,)),
+("mm", (3, 4, 1, 0,)),
+("qb", (0, 2,)),
+("mm", (3, 5, 1, 0,)),
+("mm", (7, 2, 1, 1,)),
+("mm", (5, 5, 1, 1,)),
+("sc", (1, 1, 0, 1,)),
 ("mm", (7, 3, 1, 1,)),
-("mm", (7, 4, 1, 1,)),
-("sc", (6, 1, 0, 1,)),
-("mm", (7, 5, 1, 1,)),
-("st", (5, 1, 0, 1,)),
+("mm", (4, 4, 1, 1,)),
+("qb", (2, 2,)),
+("mm", (4, 5, 1, 1,)),
+("ms", (4, 2, 160,)),
 ("mm", (0, 0, 2, 0,)),
-("mv", (5, 2, 208,)),
+("sc", (2, 1, 0, 1,)),
 ("mm", (1, 0, 2, 0,)),
-("st", (6, 1, 0, 1,)),
-("mm", (2, 0, 2, 0,)),
-("sc", (7, 1, 0, 1,)),
-("mm", (3, 0, 2, 0,)),
-("mm", (4, 0, 2, 1,)),
-("qb", (5, 2,)),
-("mm", (5, 0, 2, 1,)),
-("st", (7, 1, 0, 1,)),
-("mm", (6, 0, 2, 1,)),
-("mm", (7, 0, 2, 1,)),
-("mm", (0, 1, 2, 0,)),
+("mm", (7, 4, 1, 1,)),
+("mv", (3, 2, 160,)),
+("st", (2, 1, 0, 1,)),
+("st", (0, 1, 0, 1,)),
 ("mm", (1, 1, 2, 0,)),
+("st", (1, 1, 0, 1,)),
+("sc", (3, 1, 0, 1,)),
+("mm", (2, 0, 2, 0,)),
+("mm", (6, 5, 1, 1,)),
+("ms", (5, 2, 160,)),
+("sc", (4, 1, 0, 1,)),
+("mm", (0, 1, 2, 0,)),
+("st", (3, 1, 0, 1,)),
+("mm", (1, 2, 2, 0,)),
+("sc", (5, 1, 0, 1,)),
+("mm", (3, 0, 2, 0,)),
+("mm", (0, 2, 2, 0,)),
+("mv", (4, 2, 160,)),
 ("mm", (2, 1, 2, 0,)),
 ("mm", (3, 1, 2, 0,)),
-("mm", (4, 1, 2, 1,)),
-("mm", (5, 1, 2, 1,)),
-("mm", (6, 1, 2, 1,)),
-("mm", (7, 1, 2, 1,)),
-("mm", (0, 2, 2, 0,)),
-("mm", (1, 2, 2, 0,)),
-("mm", (2, 2, 2, 0,)),
+("qb", (3, 2,)),
+("mm", (4, 0, 2, 1,)),
+("mm", (7, 5, 1, 1,)),
+("qb", (4, 2,)),
 ("mm", (3, 2, 2, 0,)),
-("mm", (4, 2, 2, 1,)),
-("mm", (5, 2, 2, 1,)),
-("mm", (6, 2, 2, 1,)),
-("mm", (7, 2, 2, 1,)),
+("mm", (2, 2, 2, 0,)),
+("mv", (5, 2, 160,)),
 ("mm", (0, 3, 2, 0,)),
+("sc", (6, 1, 0, 1,)),
+("mm", (4, 1, 2, 1,)),
+("mm", (1, 3, 2, 0,)),
+("qb", (5, 2,)),
+("mm", (4, 2, 2, 1,)),
+("st", (6, 1, 0, 1,)),
+("st", (4, 1, 0, 1,)),
+("mm", (5, 0, 2, 1,)),
+("st", (5, 1, 0, 1,)),
+("mm", (4, 3, 2, 1,)),
+("sc", (7, 1, 0, 1,)),
+("mm", (1, 4, 2, 0,)),
+("mm", (6, 0, 2, 1,)),
 ("mm", (0, 4, 2, 0,)),
 ("mm", (0, 5, 2, 0,)),
-("mm", (1, 3, 2, 0,)),
+("mm", (3, 3, 2, 0,)),
 ("sc", (0, 2, 0, 1,)),
-("mm", (1, 4, 2, 0,)),
 ("mm", (1, 5, 2, 0,)),
 ("mm", (2, 3, 2, 0,)),
-("st", (0, 2, 0, 1,)),
 ("sc", (1, 2, 0, 1,)),
+("mm", (3, 4, 2, 0,)),
 ("mm", (2, 4, 2, 0,)),
 ("mm", (2, 5, 2, 0,)),
-("mm", (3, 3, 2, 0,)),
 ("st", (1, 2, 0, 1,)),
+("st", (7, 1, 0, 1,)),
+("st", (0, 2, 0, 1,)),
+("mm", (7, 0, 2, 1,)),
 ("sc", (2, 2, 0, 1,)),
-("mm", (3, 4, 2, 0,)),
 ("mm", (3, 5, 2, 0,)),
-("mm", (4, 3, 2, 1,)),
-("st", (2, 2, 0, 1,)),
+("mm", (5, 1, 2, 1,)),
 ("sc", (3, 2, 0, 1,)),
 ("mm", (4, 4, 2, 1,)),
+("st", (2, 2, 0, 1,)),
+("mm", (7, 1, 2, 1,)),
+("mm", (5, 2, 2, 1,)),
+("st", (3, 2, 0, 1,)),
 ("mm", (4, 5, 2, 1,)),
 ("mm", (5, 3, 2, 1,)),
-("st", (3, 2, 0, 1,)),
 ("sc", (4, 2, 0, 1,)),
+("mm", (6, 1, 2, 1,)),
 ("mm", (5, 4, 2, 1,)),
+("mm", (6, 2, 2, 1,)),
+("st", (4, 2, 0, 1,)),
 ("mm", (5, 5, 2, 1,)),
 ("mm", (6, 3, 2, 1,)),
-("st", (4, 2, 0, 1,)),
 ("sc", (5, 2, 0, 1,)),
 ("mm", (6, 4, 2, 1,)),
 ("mm", (6, 5, 2, 1,)),
-("mm", (7, 3, 2, 1,)),
+("mm", (7, 2, 2, 1,)),
 ("st", (5, 2, 0, 1,)),
 ("sc", (6, 2, 0, 1,)),
+("mm", (7, 3, 2, 1,)),
 ("mm", (7, 4, 2, 1,)),
 ("mm", (7, 5, 2, 1,)),
 ("st", (6, 2, 0, 1,)),
-("sc", (7, 2, 0, 2,)),
 ("sc", (7, 2, 1, 2,)),
-("st", (7, 2, 0, 2,)),
-("st", (7, 2, 1, 2,))])
+("sc", (7, 2, 0, 2,)),
+("st", (7, 2, 1, 2,)),
+("st", (7, 2, 0, 2,))])
         with tc.manual_schedule():
             with tc.psum_pool(name="tp", bufs=TP) as tp_pool:
                 tp[0] = tp_pool

@@ -29,11 +29,11 @@ def tile_rp3beta_item_walk_s2_kernel(tc, iu, ui, iv, vi, pop, out):
     nc = tc.nc
     with ExitStack() as ctx:
         const = ctx.enter_context(tc.tile_pool(name="const", bufs=1))
-        araw_pool = ctx.enter_context(tc.tile_pool(name="araw", bufs=8))
+        araw_pool = ctx.enter_context(tc.tile_pool(name="araw", bufs=6))
         agrp_pool = ctx.enter_context(tc.tile_pool(name="agrp", bufs=3))
         aperm_pool = ctx.enter_context(tc.tile_pool(name="aperm", bufs=4))
         codes_pool = ctx.enter_context(tc.tile_pool(name="codes", bufs=1))
-        braw_pool = ctx.enter_context(tc.tile_pool(name="braw", bufs=10))
+        braw_pool = ctx.enter_context(tc.tile_pool(name="braw", bufs=13))
         bgrp_pool = ctx.enter_context(tc.tile_pool(name="bgrp", bufs=4))
         res_pool = ctx.enter_context(tc.tile_pool(name="res", bufs=6))
         acc_pool = ctx.enter_context(tc.psum_pool(name="acc", bufs=4))
@@ -120,8 +120,8 @@ def tile_rp3beta_item_walk_s2_kernel(tc, iu, ui, iv, vi, pop, out):
 
         def quant_a(m, part):
             if m not in a_codes:
-                a_codes[m] = codes_pool.tile([P, PASSES * P], U32, name="a_codes%d" % m, align_bytes=64)
-                a_scales[m] = codes_pool.tile([P, PASSES * P], U8, name="a_scales%d" % m, align_bytes=64)
+                a_codes[m] = codes_pool.tile([P, PASSES * P], U32, name="a_codes%d" % m, align_bytes=256)
+                a_scales[m] = codes_pool.tile([P, PASSES * P], U8, name="a_scales%d" % m, align_bytes=256)
             flat = a_grp[m][:].rearrange("p g r t -> p (g r t)")
             split = U_PASSES * P
             cols = slice(0, split) if part == 0 else slice(split, PASSES * P)
@@ -143,8 +143,8 @@ def tile_rp3beta_item_walk_s2_kernel(tc, iu, ui, iv, vi, pop, out):
                 nc.scalar.copy(out=dst[:, x // 4 :], in_=src[:, x // 4 :])
 
         def quant_b(g, n):
-            b_codes[g, n] = codes_pool.tile([P, N_TILE], U32, name="b_codes%d_%d" % (g, n), align_bytes=64)
-            b_scales[g, n] = codes_pool.tile([P, N_TILE], U8, name="b_scales%d_%d" % (g, n), align_bytes=64)
+            b_codes[g, n] = codes_pool.tile([P, N_TILE], U32, name="b_codes%d_%d" % (g, n), align_bytes=256)
+            b_scales[g, n] = codes_pool.tile([P, N_TILE], U8, name="b_scales%d_%d" % (g, n), align_bytes=256)
             nc.vector.quantize_mx(
                 out=b_codes[g, n][:].bitcast(E4M3X4),
                 scales=b_scales[g, n][:],
@@ -217,359 +217,353 @@ def tile_rp3beta_item_walk_s2_kernel(tc, iu, ui, iv, vi, pop, out):
             elif name == "st":
                 store(a[0], a[1], a[2], a[3])
 
-        part1, part2 = ([("lb", (0, 0,)),
-("la", (0, 2,)),
+        part1, part2 = ([("la", (0, 2,)),
 ("la", (1, 1,)),
-("lb", (1, 0,)),
+("lb", (0, 0,)),
 ("la", (2, 1,)),
-("ms", (0, 0, 256,)),
-("la", (3, 1,)),
-("pa", (0, 0,)),
-("mv", (0, 0, 256,)),
+("lb", (1, 0,)),
 ("tu", (0, 0,)),
-("pa", (0, 1,)),
-("lb", (2, 0,)),
-("ev", (0, 0, 0,)),
-("pa", (0, 2,)),
+("la", (3, 1,)),
 ("tu", (0, 1,)),
+("ev", (0, 0, 0,)),
 ("tu", (0, 2,)),
-("ev", (0, 1, 0,)),
-("lb", (3, 0,)),
-("pa", (1, 0,)),
-("qb", (0, 0,)),
-("ev", (0, 2, 0,)),
+("lb", (2, 0,)),
 ("tu", (1, 0,)),
-("lb", (4, 0,)),
-("pa", (1, 1,)),
-("qa", (0, 0,)),
-("ev", (1, 0, 0,)),
+("ev", (0, 2, 0,)),
+("lb", (3, 0,)),
+("ev", (0, 1, 0,)),
 ("tu", (1, 1,)),
-("pa", (1, 2,)),
-("la", (4, 1,)),
 ("qa", (0, 1,)),
-("ms", (1, 0, 256,)),
+("ev", (1, 0, 0,)),
+("qa", (0, 0,)),
 ("tu", (1, 2,)),
-("mv", (1, 0, 256,)),
+("la", (4, 1,)),
+("ms", (0, 0, 288,)),
+("mv", (0, 0, 288,)),
+("ev", (1, 1, 0,)),
 ("pa", (2, 0,)),
-("ev", (1, 2, 0,)),
 ("pa", (2, 1,)),
 ("tu", (2, 0,)),
-("lb", (5, 0,)),
-("qb", (1, 0,)),
-("ev", (1, 1, 0,)),
-("tu", (2, 1,)),
+("ev", (1, 2, 0,)),
+("lb", (4, 0,)),
 ("pa", (2, 2,)),
+("qb", (0, 0,)),
+("tu", (2, 1,)),
 ("ev", (2, 0, 0,)),
+("qa", (1, 0,)),
+("mm", (0, 0, 0, 0,)),
+("ev", (2, 1, 0,)),
+("lb", (5, 0,)),
 ("qa", (1, 1,)),
+("mm", (1, 0, 0, 0,)),
+("ms", (1, 0, 272,)),
+("mv", (1, 0, 272,)),
 ("tu", (2, 2,)),
 ("la", (5, 1,)),
-("ev", (2, 1, 0,)),
 ("pa", (3, 0,)),
 ("pa", (3, 1,)),
 ("tu", (3, 0,)),
-("qa", (1, 0,)),
 ("ev", (2, 2, 0,)),
+("qa", (2, 0,)),
 ("tu", (3, 1,)),
 ("pa", (3, 2,)),
 ("ev", (3, 0, 0,)),
-("qa", (2, 1,)),
-("mm", (0, 0, 0, 0,)),
-("qa", (2, 0,)),
-("ev", (3, 1, 0,)),
-("lb", (1, 1,)),
-("mm", (1, 0, 0, 0,)),
-("mv", (2, 0, 256,)),
-("ms", (2, 0, 256,)),
-("mm", (0, 1, 0, 0,)),
-("qa", (3, 0,)),
-("mm", (1, 1, 0, 0,)),
-("la", (6, 1,)),
-("ms", (3, 0, 256,)),
-("mv", (3, 0, 256,)),
+("qb", (1, 0,)),
 ("tu", (3, 2,)),
+("ev", (3, 1, 0,)),
 ("pw", (0,)),
-("qb", (2, 0,)),
+("la", (6, 1,)),
+("mv", (2, 0, 208,)),
 ("pw", (1,)),
-("pw", (2,)),
-("mv", (4, 0, 256,)),
-("ms", (4, 0, 256,)),
-("mm", (2, 0, 0, 0,)),
-("mm", (3, 0, 0, 0,)),
-("qb", (3, 0,)),
-("mm", (1, 2, 0, 0,)),
-("lb", (0, 1,)),
-("mm", (3, 1, 0, 0,)),
-("ev", (3, 2, 0,)),
-("pa", (4, 0,)),
-("mm", (0, 2, 0, 0,)),
+("ms", (2, 0, 208,)),
 ("gw", (0,)),
-("mm", (1, 3, 0, 0,)),
-("la", (7, 1,)),
+("mm", (2, 0, 0, 0,)),
+("mm", (0, 1, 0, 0,)),
+("gw", (1,)),
+("mm", (1, 1, 0, 0,)),
+("pw", (2,)),
+("qa", (3, 0,)),
+("ms", (3, 0, 64,)),
 ("mm", (2, 1, 0, 0,)),
+("qb", (2, 0,)),
+("mm", (3, 0, 0, 0,)),
+("la", (7, 1,)),
+("mm", (3, 1, 0, 0,)),
+("pa", (4, 0,)),
+("mm", (1, 2, 0, 0,)),
+("mv", (3, 0, 64,)),
+("mm", (0, 2, 0, 0,)),
 ("pa", (4, 1,)),
+("mm", (3, 2, 0, 0,)),
+("gw", (2,)),
 ("mm", (2, 2, 0, 0,)),
+("ev", (3, 2, 0,)),
 ("pa", (4, 2,)),
+("qb", (3, 0,)),
+("tu", (4, 0,)),
+("lb", (0, 1,)),
+("ms", (4, 0, 288,)),
+("tu", (4, 1,)),
+("mv", (4, 0, 288,)),
+("tu", (4, 2,)),
 ("mm", (2, 3, 0, 0,)),
+("ev", (4, 0, 0,)),
+("qa", (3, 1,)),
+("mm", (1, 3, 0, 0,)),
+("lb", (5, 1,)),
 ("qb", (4, 0,)),
 ("mm", (0, 3, 0, 0,)),
-("tu", (4, 0,)),
-("ms", (5, 0, 256,)),
-("mv", (5, 0, 256,)),
-("tu", (4, 1,)),
-("gw", (1,)),
-("mm", (1, 4, 0, 0,)),
-("mm", (0, 4, 0, 0,)),
-("ev", (4, 0, 0,)),
-("qb", (5, 0,)),
-("tu", (4, 2,)),
-("ev", (4, 1, 0,)),
-("mm", (2, 4, 0, 0,)),
-("gw", (2,)),
-("mm", (3, 2, 0, 0,)),
-("ev", (4, 2, 0,)),
-("mm", (0, 5, 0, 0,)),
-("pa", (5, 0,)),
+("ms", (5, 0, 160,)),
 ("mm", (3, 3, 0, 0,)),
+("qa", (2, 1,)),
+("mm", (0, 4, 0, 0,)),
+("mv", (5, 0, 160,)),
+("mm", (3, 4, 0, 0,)),
+("mm", (2, 4, 0, 0,)),
+("pa", (5, 0,)),
+("mm", (1, 4, 0, 0,)),
 ("pa", (5, 1,)),
-("mm", (1, 5, 0, 0,)),
-("pa", (5, 2,)),
-("ms", (1, 1, 160,)),
-("mm", (2, 5, 0, 0,)),
-("qa", (4, 0,)),
+("ev", (4, 2, 0,)),
 ("tu", (5, 0,)),
-("sc", (0, 0, 0, 1,)),
+("qb", (5, 0,)),
 ("tu", (5, 1,)),
-("tu", (5, 2,)),
+("ev", (4, 1, 0,)),
+("pa", (5, 2,)),
+("mm", (1, 5, 0, 0,)),
 ("pa", (6, 0,)),
-("st", (0, 0, 0, 1,)),
-("lb", (2, 1,)),
-("mm", (4, 0, 0, 0,)),
-("pa", (6, 1,)),
-("ev", (5, 0, 0,)),
-("mm", (4, 1, 0, 0,)),
-("sc", (1, 0, 0, 1,)),
-("mm", (4, 2, 0, 0,)),
 ("ev", (5, 1, 0,)),
-("qa", (4, 1,)),
-("st", (1, 0, 0, 1,)),
+("mm", (0, 5, 0, 0,)),
+("pa", (6, 1,)),
+("mm", (3, 5, 0, 0,)),
+("ev", (5, 0, 0,)),
+("pa", (6, 2,)),
+("tu", (5, 2,)),
+("qa", (4, 0,)),
 ("tu", (6, 0,)),
-("lb", (3, 1,)),
-("lb", (4, 1,)),
 ("ev", (5, 2, 0,)),
 ("tu", (6, 1,)),
-("qa", (5, 0,)),
-("lb", (1, 2,)),
-("mm", (4, 3, 0, 0,)),
-("qa", (3, 1,)),
-("mm", (4, 4, 0, 0,)),
-("mv", (0, 1, 160,)),
-("mm", (5, 0, 0, 0,)),
-("ev", (6, 0, 0,)),
-("mm", (3, 4, 0, 0,)),
-("mv", (1, 1, 160,)),
-("lb", (5, 1,)),
-("mm", (4, 5, 0, 0,)),
-("ev", (6, 1, 0,)),
-("pa", (6, 2,)),
-("mm", (3, 5, 0, 0,)),
-("pa", (7, 0,)),
-("mm", (5, 1, 0, 0,)),
-("lb", (0, 2,)),
-("ms", (0, 1, 160,)),
-("pa", (7, 1,)),
+("sc", (0, 0, 0, 1,)),
 ("tu", (6, 2,)),
+("ev", (6, 1, 0,)),
+("qa", (4, 1,)),
+("mm", (2, 5, 0, 0,)),
+("st", (0, 0, 0, 1,)),
+("lb", (1, 1,)),
+("pa", (7, 0,)),
+("mm", (4, 0, 0, 0,)),
+("ev", (6, 0, 0,)),
+("pa", (7, 1,)),
+("mm", (4, 1, 0, 0,)),
 ("pa", (7, 2,)),
-("lb", (2, 2,)),
+("mm", (4, 2, 0, 0,)),
+("ev", (6, 2, 0,)),
+("sc", (1, 0, 0, 1,)),
 ("tu", (7, 0,)),
-("qa", (6, 0,)),
 ("tu", (7, 1,)),
-("tu", (7, 2,)),
-("sc", (2, 0, 0, 1,)),
-("ev", (7, 1, 0,)),
-("mm", (5, 2, 0, 0,)),
-("qb", (0, 1,)),
-("mm", (5, 3, 0, 0,)),
+("qa", (5, 0,)),
+("st", (1, 0, 0, 1,)),
 ("ev", (7, 0, 0,)),
-("mm", (6, 0, 0, 0,)),
-("qa", (5, 1,)),
-("mm", (6, 1, 0, 0,)),
+("lb", (2, 1,)),
+("tu", (7, 2,)),
+("lb", (1, 2,)),
+("sc", (2, 0, 0, 1,)),
+("mm", (4, 3, 0, 0,)),
 ("ev", (7, 2, 0,)),
+("mm", (4, 4, 0, 0,)),
 ("sc", (3, 0, 0, 1,)),
-("mm", (6, 2, 0, 0,)),
-("mm", (6, 3, 0, 0,)),
-("ev", (6, 2, 0,))],
-[("qa", (7, 0,)),
-("mm", (4, 0, 1, 1,)),
-("mm", (5, 0, 1, 1,)),
-("ms", (2, 1, 160,)),
-("mv", (2, 1, 160,)),
-("mm", (5, 4, 0, 0,)),
-("mm", (5, 5, 0, 0,)),
+("mm", (4, 5, 0, 0,)),
+("ev", (7, 1, 0,))],
+[("mm", (5, 0, 0, 0,)),
+("qa", (5, 1,)),
+("mm", (5, 1, 0, 0,)),
+("ms", (0, 1, 64,)),
+("qa", (6, 0,)),
+("mm", (5, 2, 0, 0,)),
+("mm", (5, 3, 0, 0,)),
 ("qa", (6, 1,)),
-("mm", (6, 0, 1, 1,)),
-("sc", (4, 0, 0, 1,)),
-("mm", (7, 0, 0, 0,)),
-("mm", (7, 1, 0, 0,)),
-("qb", (1, 1,)),
-("mm", (6, 4, 0, 0,)),
-("ms", (3, 1, 160,)),
-("mm", (6, 5, 0, 0,)),
-("qb", (2, 1,)),
-("mm", (0, 0, 1, 0,)),
-("mm", (7, 2, 0, 0,)),
-("sc", (5, 0, 0, 1,)),
-("mm", (5, 1, 1, 1,)),
-("mm", (7, 0, 1, 1,)),
+("mm", (5, 4, 0, 0,)),
+("qa", (7, 0,)),
+("mm", (5, 5, 0, 0,)),
+("mm", (6, 0, 0, 0,)),
 ("qa", (7, 1,)),
-("st", (5, 0, 0, 1,)),
+("mm", (6, 1, 0, 0,)),
+("mv", (0, 1, 64,)),
+("mm", (6, 2, 0, 0,)),
+("sc", (4, 0, 0, 1,)),
+("mm", (6, 3, 0, 0,)),
+("ms", (1, 1, 64,)),
+("mm", (7, 0, 0, 0,)),
+("qb", (0, 1,)),
+("st", (4, 0, 0, 1,)),
+("mm", (7, 1, 0, 0,)),
+("lb", (3, 1,)),
+("lb", (4, 1,)),
+("mm", (7, 2, 0, 0,)),
+("lb", (0, 2,)),
+("lb", (2, 2,)),
+("sc", (5, 0, 0, 1,)),
+("st", (3, 0, 0, 1,)),
 ("mm", (7, 3, 0, 0,)),
-("mv", (3, 1, 160,)),
-("ms", (4, 1, 160,)),
-("mm", (6, 1, 1, 1,)),
-("mm", (6, 2, 1, 1,)),
-("mv", (4, 1, 160,)),
-("mm", (4, 1, 1, 1,)),
-("qb", (3, 1,)),
-("mm", (1, 0, 1, 0,)),
-("mm", (0, 1, 1, 0,)),
-("sc", (6, 0, 0, 1,)),
+("mm", (6, 4, 0, 0,)),
+("mv", (1, 1, 64,)),
+("mm", (6, 5, 0, 0,)),
+("mv", (2, 1, 112,)),
+("mm", (4, 0, 1, 1,)),
+("ms", (2, 1, 112,)),
+("mm", (5, 0, 1, 1,)),
+("qb", (1, 1,)),
 ("mm", (7, 4, 0, 0,)),
-("ms", (1, 2, 160,)),
-("mm", (0, 2, 1, 0,)),
-("qb", (4, 1,)),
-("mm", (4, 2, 1, 1,)),
+("mm", (0, 0, 1, 0,)),
+("sc", (6, 0, 0, 1,)),
+("mm", (6, 0, 1, 1,)),
 ("mm", (7, 5, 0, 0,)),
-("mm", (0, 3, 1, 0,)),
+("mm", (7, 0, 1, 1,)),
 ("sc", (7, 0, 0, 1,)),
-("mm", (5, 2, 1, 1,)),
-("mm", (5, 3, 1, 1,)),
-("mv", (5, 1, 160,)),
-("ms", (5, 1, 160,)),
-("mm", (2, 0, 1, 0,)),
+("mm", (4, 1, 1, 1,)),
+("ms", (5, 1, 240,)),
+("mm", (1, 0, 1, 0,)),
+("qb", (2, 1,)),
+("mm", (6, 1, 1, 1,)),
 ("st", (7, 0, 0, 1,)),
 ("st", (2, 0, 0, 1,)),
-("st", (3, 0, 0, 1,)),
-("mm", (1, 1, 1, 0,)),
 ("lb", (3, 2,)),
-("mv", (0, 2, 160,)),
-("st", (4, 0, 0, 1,)),
-("mm", (0, 4, 1, 0,)),
-("st", (6, 0, 0, 1,)),
-("lb", (4, 2,)),
-("mv", (1, 2, 160,)),
-("mm", (2, 1, 1, 0,)),
+("mm", (0, 1, 1, 0,)),
+("st", (5, 0, 0, 1,)),
+("mm", (2, 0, 1, 0,)),
+("mv", (3, 1, 384,)),
+("mm", (5, 1, 1, 1,)),
+("ms", (3, 1, 384,)),
 ("mm", (3, 0, 1, 0,)),
-("lb", (5, 2,)),
-("mm", (2, 2, 1, 0,)),
-("mm", (2, 3, 1, 0,)),
-("ms", (0, 2, 160,)),
-("qb", (5, 1,)),
-("mm", (1, 2, 1, 0,)),
-("mm", (5, 4, 1, 1,)),
-("mv", (2, 2, 160,)),
-("mm", (1, 3, 1, 0,)),
-("mm", (2, 4, 1, 0,)),
-("mm", (4, 3, 1, 1,)),
-("mm", (3, 1, 1, 0,)),
-("ms", (2, 2, 160,)),
-("mm", (3, 2, 1, 0,)),
-("mm", (3, 3, 1, 0,)),
-("mm", (6, 3, 1, 1,)),
-("mm", (1, 4, 1, 0,)),
-("mm", (0, 5, 1, 0,)),
 ("mm", (7, 1, 1, 1,)),
-("ms", (3, 2, 160,)),
-("sc", (0, 1, 0, 1,)),
-("mm", (2, 5, 1, 0,)),
-("mm", (6, 4, 1, 1,)),
-("qb", (1, 2,)),
-("mm", (1, 5, 1, 0,)),
-("mm", (3, 4, 1, 0,)),
-("qb", (0, 2,)),
-("mm", (3, 5, 1, 0,)),
+("mm", (1, 1, 1, 0,)),
+("st", (6, 0, 0, 1,)),
+("mm", (1, 2, 1, 0,)),
+("mv", (4, 1, 80,)),
+("ms", (4, 1, 80,)),
 ("mm", (7, 2, 1, 1,)),
+("qb", (3, 1,)),
+("mm", (6, 2, 1, 1,)),
+("mm", (3, 1, 1, 0,)),
+("mv", (5, 1, 240,)),
+("mm", (3, 2, 1, 0,)),
+("mm", (4, 2, 1, 1,)),
+("lb", (4, 2,)),
+("mv", (0, 2, 112,)),
+("mm", (2, 1, 1, 0,)),
+("mm", (0, 2, 1, 0,)),
+("ms", (0, 2, 112,)),
+("mm", (1, 3, 1, 0,)),
+("qb", (4, 1,)),
+("mm", (4, 3, 1, 1,)),
+("mm", (2, 2, 1, 0,)),
+("qb", (5, 1,)),
+("mm", (2, 3, 1, 0,)),
+("mm", (3, 3, 1, 0,)),
+("mv", (1, 2, 416,)),
+("mm", (7, 3, 1, 1,)),
+("mm", (0, 3, 1, 0,)),
+("ms", (1, 2, 416,)),
+("mm", (1, 4, 1, 0,)),
+("mm", (0, 4, 1, 0,)),
+("mv", (2, 2, 64,)),
+("ms", (2, 2, 64,)),
+("qb", (0, 2,)),
+("mm", (5, 2, 1, 1,)),
+("mm", (2, 4, 1, 0,)),
+("qb", (1, 2,)),
+("mm", (5, 3, 1, 1,)),
+("mm", (3, 4, 1, 0,)),
+("mm", (5, 4, 1, 1,)),
+("mm", (0, 5, 1, 0,)),
+("mm", (1, 5, 1, 0,)),
+("sc", (0, 1, 0, 1,)),
+("mm", (6, 3, 1, 1,)),
+("ms", (3, 2, 80,)),
 ("mm", (5, 5, 1, 1,)),
 ("sc", (1, 1, 0, 1,)),
-("mm", (7, 3, 1, 1,)),
-("mm", (4, 4, 1, 1,)),
-("qb", (2, 2,)),
-("mm", (4, 5, 1, 1,)),
-("ms", (4, 2, 160,)),
+("mm", (6, 4, 1, 1,)),
+("st", (0, 1, 0, 1,)),
+("mm", (3, 5, 1, 0,)),
+("mv", (3, 2, 80,)),
+("mm", (2, 5, 1, 0,)),
+("st", (1, 1, 0, 1,)),
+("lb", (5, 2,)),
 ("mm", (0, 0, 2, 0,)),
 ("sc", (2, 1, 0, 1,)),
+("mm", (4, 4, 1, 1,)),
+("mm", (4, 5, 1, 1,)),
+("sc", (3, 1, 0, 1,)),
+("ms", (4, 2, 192,)),
 ("mm", (1, 0, 2, 0,)),
 ("mm", (7, 4, 1, 1,)),
-("mv", (3, 2, 160,)),
-("st", (2, 1, 0, 1,)),
-("st", (0, 1, 0, 1,)),
-("mm", (1, 1, 2, 0,)),
-("st", (1, 1, 0, 1,)),
-("sc", (3, 1, 0, 1,)),
-("mm", (2, 0, 2, 0,)),
-("mm", (6, 5, 1, 1,)),
-("ms", (5, 2, 160,)),
-("sc", (4, 1, 0, 1,)),
+("qb", (2, 2,)),
 ("mm", (0, 1, 2, 0,)),
-("st", (3, 1, 0, 1,)),
-("mm", (1, 2, 2, 0,)),
-("sc", (5, 1, 0, 1,)),
-("mm", (3, 0, 2, 0,)),
-("mm", (0, 2, 2, 0,)),
-("mv", (4, 2, 160,)),
-("mm", (2, 1, 2, 0,)),
-("mm", (3, 1, 2, 0,)),
-("qb", (3, 2,)),
-("mm", (4, 0, 2, 1,)),
+("mm", (2, 0, 2, 0,)),
+("sc", (4, 1, 0, 1,)),
 ("mm", (7, 5, 1, 1,)),
-("qb", (4, 2,)),
-("mm", (3, 2, 2, 0,)),
-("mm", (2, 2, 2, 0,)),
-("mv", (5, 2, 160,)),
-("mm", (0, 3, 2, 0,)),
-("sc", (6, 1, 0, 1,)),
-("mm", (4, 1, 2, 1,)),
-("mm", (1, 3, 2, 0,)),
-("qb", (5, 2,)),
-("mm", (4, 2, 2, 1,)),
-("st", (6, 1, 0, 1,)),
-("st", (4, 1, 0, 1,)),
-("mm", (5, 0, 2, 1,)),
+("mm", (2, 1, 2, 0,)),
+("sc", (5, 1, 0, 1,)),
+("mm", (1, 1, 2, 0,)),
+("mm", (3, 0, 2, 0,)),
+("mv", (4, 2, 192,)),
+("mm", (1, 2, 2, 0,)),
 ("st", (5, 1, 0, 1,)),
-("mm", (4, 3, 2, 1,)),
-("sc", (7, 1, 0, 1,)),
-("mm", (1, 4, 2, 0,)),
-("mm", (6, 0, 2, 1,)),
-("mm", (0, 4, 2, 0,)),
-("mm", (0, 5, 2, 0,)),
-("mm", (3, 3, 2, 0,)),
-("sc", (0, 2, 0, 1,)),
-("mm", (1, 5, 2, 0,)),
+("st", (2, 1, 0, 1,)),
+("mm", (4, 0, 2, 1,)),
+("st", (3, 1, 0, 1,)),
+("st", (4, 1, 0, 1,)),
+("qb", (3, 2,)),
+("mm", (0, 2, 2, 0,)),
+("ms", (5, 2, 352,)),
+("mm", (2, 2, 2, 0,)),
+("qb", (4, 2,)),
+("mm", (6, 5, 1, 1,)),
+("mm", (3, 1, 2, 0,)),
+("mv", (5, 2, 352,)),
+("mm", (5, 0, 2, 1,)),
+("mm", (3, 2, 2, 0,)),
 ("mm", (2, 3, 2, 0,)),
-("sc", (1, 2, 0, 1,)),
-("mm", (3, 4, 2, 0,)),
+("mm", (3, 3, 2, 0,)),
 ("mm", (2, 4, 2, 0,)),
-("mm", (2, 5, 2, 0,)),
-("st", (1, 2, 0, 1,)),
+("qb", (5, 2,)),
+("mm", (3, 4, 2, 0,)),
+("mm", (4, 1, 2, 1,)),
+("sc", (6, 1, 0, 1,)),
+("mm", (0, 3, 2, 0,)),
+("mm", (1, 3, 2, 0,)),
+("sc", (7, 1, 0, 1,)),
+("st", (6, 1, 0, 1,)),
+("mm", (4, 2, 2, 1,)),
+("mm", (0, 4, 2, 0,)),
 ("st", (7, 1, 0, 1,)),
-("st", (0, 2, 0, 1,)),
-("mm", (7, 0, 2, 1,)),
-("sc", (2, 2, 0, 1,)),
-("mm", (3, 5, 2, 0,)),
 ("mm", (5, 1, 2, 1,)),
-("sc", (3, 2, 0, 1,)),
-("mm", (4, 4, 2, 1,)),
-("st", (2, 2, 0, 1,)),
-("mm", (7, 1, 2, 1,)),
+("mm", (1, 4, 2, 0,)),
+("mm", (1, 5, 2, 0,)),
 ("mm", (5, 2, 2, 1,)),
-("st", (3, 2, 0, 1,)),
-("mm", (4, 5, 2, 1,)),
+("mm", (4, 3, 2, 1,)),
+("mm", (0, 5, 2, 0,)),
+("mm", (6, 0, 2, 1,)),
+("sc", (0, 2, 0, 1,)),
+("mm", (2, 5, 2, 0,)),
 ("mm", (5, 3, 2, 1,)),
-("sc", (4, 2, 0, 1,)),
+("sc", (1, 2, 0, 1,)),
+("mm", (3, 5, 2, 0,)),
+("st", (0, 2, 0, 1,)),
 ("mm", (6, 1, 2, 1,)),
-("mm", (5, 4, 2, 1,)),
+("sc", (2, 2, 0, 1,)),
+("mm", (7, 0, 2, 1,)),
+("st", (1, 2, 0, 1,)),
+("mm", (4, 4, 2, 1,)),
+("sc", (3, 2, 0, 1,)),
+("mm", (4, 5, 2, 1,)),
+("st", (2, 2, 0, 1,)),
 ("mm", (6, 2, 2, 1,)),
-("st", (4, 2, 0, 1,)),
+("sc", (4, 2, 0, 1,)),
+("mm", (5, 4, 2, 1,)),
+("st", (3, 2, 0, 1,)),
+("mm", (7, 1, 2, 1,)),
 ("mm", (5, 5, 2, 1,)),
+("st", (4, 2, 0, 1,)),
 ("mm", (6, 3, 2, 1,)),
 ("sc", (5, 2, 0, 1,)),
 ("mm", (6, 4, 2, 1,)),

@@ -22,7 +22,6 @@ N_TILE = 512
 N_TILES = N // N_TILE
 BETA = 0.6
 POP_COLS = N // P
-TP = 4
 
 
 def tile_rp3beta_item_walk_s2_kernel(tc, iu, ui, iv, vi, pop, out):
@@ -35,7 +34,7 @@ def tile_rp3beta_item_walk_s2_kernel(tc, iu, ui, iv, vi, pop, out):
         codes_pool = ctx.enter_context(tc.tile_pool(name="codes", bufs=1))
         braw_pool = ctx.enter_context(tc.tile_pool(name="braw", bufs=13))
         bgrp_pool = ctx.enter_context(tc.tile_pool(name="bgrp", bufs=4))
-        res_pool = ctx.enter_context(tc.tile_pool(name="res", bufs=6))
+        res_pool = ctx.enter_context(tc.tile_pool(name="res", bufs=8))
         acc_pool = ctx.enter_context(tc.psum_pool(name="acc", bufs=4))
 
         pop_sb = const.tile([P, POP_COLS], BF16, name="pop_sb")
@@ -185,405 +184,145 @@ def tile_rp3beta_item_walk_s2_kernel(tc, iu, ui, iv, vi, pop, out):
             )
 
 
-        tp = [None]
+        X = {0: (400, 208, 208, 144, 144, 208), 1: 208, 2: 240}
 
-        def run(name, a):
-            if name == "la":
-                load_a(a[0], a[1])
-            elif name == "lb":
-                load_b(a[0], a[1])
-            elif name == "pw":
-                spread_pop(a[0], tp[0])
-            elif name == "gw":
-                gather_pop(a[0])
-            elif name == "pa":
-                permute_a(a[0], a[1])
-            elif name == "tu":
-                turn_a(a[0], a[1], tp[0])
-            elif name == "ev":
-                evac_a(a[0], a[1], nc.scalar.copy if a[2] == 0 else nc.vector.tensor_copy)
-            elif name == "qa":
-                quant_a(a[0], a[1])
-            elif name == "mv":
-                mix_b(a[0], a[1], a[2], True)
-            elif name == "ms":
-                mix_b(a[0], a[1], a[2], False)
-            elif name == "qb":
-                quant_b(a[0], a[1])
-            elif name == "mm":
-                multiply(a[0], a[1], a[2], acc_pool if a[3] == 0 else acc2_pool)
-            elif name == "sc":
-                scale(a[0], a[1], a[2], a[3])
-            elif name == "st":
-                store(a[0], a[1], a[2], a[3])
+        def permute(m):
+            if m in range(8):
+                for q in range(3):
+                    permute_a(m, q)
 
-        part1, part2 = ([("la", (0, 2,)),
-("la", (1, 1,)),
-("lb", (0, 0,)),
-("la", (2, 1,)),
-("lb", (1, 0,)),
-("tu", (0, 0,)),
-("la", (3, 1,)),
-("tu", (0, 1,)),
-("ev", (0, 0, 0,)),
-("tu", (0, 2,)),
-("lb", (2, 0,)),
-("tu", (1, 0,)),
-("ev", (0, 2, 0,)),
-("lb", (3, 0,)),
-("ev", (0, 1, 0,)),
-("tu", (1, 1,)),
-("qa", (0, 1,)),
-("ev", (1, 0, 0,)),
-("qa", (0, 0,)),
-("tu", (1, 2,)),
-("la", (4, 1,)),
-("ms", (0, 0, 288,)),
-("mv", (0, 0, 288,)),
-("ev", (1, 1, 0,)),
-("pa", (2, 0,)),
-("pa", (2, 1,)),
-("tu", (2, 0,)),
-("ev", (1, 2, 0,)),
-("lb", (4, 0,)),
-("pa", (2, 2,)),
-("qb", (0, 0,)),
-("tu", (2, 1,)),
-("ev", (2, 0, 0,)),
-("qa", (1, 0,)),
-("mm", (0, 0, 0, 0,)),
-("ev", (2, 1, 0,)),
-("lb", (5, 0,)),
-("qa", (1, 1,)),
-("mm", (1, 0, 0, 0,)),
-("ms", (1, 0, 272,)),
-("mv", (1, 0, 272,)),
-("tu", (2, 2,)),
-("la", (5, 1,)),
-("pa", (3, 0,)),
-("pa", (3, 1,)),
-("tu", (3, 0,)),
-("ev", (2, 2, 0,)),
-("qa", (2, 0,)),
-("tu", (3, 1,)),
-("pa", (3, 2,)),
-("ev", (3, 0, 0,)),
-("qb", (1, 0,)),
-("tu", (3, 2,)),
-("ev", (3, 1, 0,)),
-("pw", (0,)),
-("la", (6, 1,)),
-("mv", (2, 0, 208,)),
-("pw", (1,)),
-("ms", (2, 0, 208,)),
-("gw", (0,)),
-("mm", (2, 0, 0, 0,)),
-("mm", (0, 1, 0, 0,)),
-("gw", (1,)),
-("mm", (1, 1, 0, 0,)),
-("pw", (2,)),
-("qa", (3, 0,)),
-("ms", (3, 0, 64,)),
-("mm", (2, 1, 0, 0,)),
-("qb", (2, 0,)),
-("mm", (3, 0, 0, 0,)),
-("la", (7, 1,)),
-("mm", (3, 1, 0, 0,)),
-("pa", (4, 0,)),
-("mm", (1, 2, 0, 0,)),
-("mv", (3, 0, 64,)),
-("mm", (0, 2, 0, 0,)),
-("pa", (4, 1,)),
-("mm", (3, 2, 0, 0,)),
-("gw", (2,)),
-("mm", (2, 2, 0, 0,)),
-("ev", (3, 2, 0,)),
-("pa", (4, 2,)),
-("qb", (3, 0,)),
-("tu", (4, 0,)),
-("lb", (0, 1,)),
-("ms", (4, 0, 288,)),
-("tu", (4, 1,)),
-("mv", (4, 0, 288,)),
-("tu", (4, 2,)),
-("mm", (2, 3, 0, 0,)),
-("ev", (4, 0, 0,)),
-("qa", (3, 1,)),
-("mm", (1, 3, 0, 0,)),
-("lb", (5, 1,)),
-("qb", (4, 0,)),
-("mm", (0, 3, 0, 0,)),
-("ms", (5, 0, 160,)),
-("mm", (3, 3, 0, 0,)),
-("qa", (2, 1,)),
-("mm", (0, 4, 0, 0,)),
-("mv", (5, 0, 160,)),
-("mm", (3, 4, 0, 0,)),
-("mm", (2, 4, 0, 0,)),
-("pa", (5, 0,)),
-("mm", (1, 4, 0, 0,)),
-("pa", (5, 1,)),
-("ev", (4, 2, 0,)),
-("tu", (5, 0,)),
-("qb", (5, 0,)),
-("tu", (5, 1,)),
-("ev", (4, 1, 0,)),
-("pa", (5, 2,)),
-("mm", (1, 5, 0, 0,)),
-("pa", (6, 0,)),
-("ev", (5, 1, 0,)),
-("mm", (0, 5, 0, 0,)),
-("pa", (6, 1,)),
-("mm", (3, 5, 0, 0,)),
-("ev", (5, 0, 0,)),
-("pa", (6, 2,)),
-("tu", (5, 2,)),
-("qa", (4, 0,)),
-("tu", (6, 0,)),
-("ev", (5, 2, 0,)),
-("tu", (6, 1,)),
-("sc", (0, 0, 0, 1,)),
-("tu", (6, 2,)),
-("ev", (6, 1, 0,)),
-("qa", (4, 1,)),
-("mm", (2, 5, 0, 0,)),
-("st", (0, 0, 0, 1,)),
-("lb", (1, 1,)),
-("pa", (7, 0,)),
-("mm", (4, 0, 0, 0,)),
-("ev", (6, 0, 0,)),
-("pa", (7, 1,)),
-("mm", (4, 1, 0, 0,)),
-("pa", (7, 2,)),
-("mm", (4, 2, 0, 0,)),
-("ev", (6, 2, 0,)),
-("sc", (1, 0, 0, 1,)),
-("tu", (7, 0,)),
-("tu", (7, 1,)),
-("qa", (5, 0,)),
-("st", (1, 0, 0, 1,)),
-("ev", (7, 0, 0,)),
-("lb", (2, 1,)),
-("tu", (7, 2,)),
-("lb", (1, 2,)),
-("sc", (2, 0, 0, 1,)),
-("mm", (4, 3, 0, 0,)),
-("ev", (7, 2, 0,)),
-("mm", (4, 4, 0, 0,)),
-("sc", (3, 0, 0, 1,)),
-("mm", (4, 5, 0, 0,)),
-("ev", (7, 1, 0,))],
-[("mm", (5, 0, 0, 0,)),
-("qa", (5, 1,)),
-("mm", (5, 1, 0, 0,)),
-("ms", (0, 1, 64,)),
-("qa", (6, 0,)),
-("mm", (5, 2, 0, 0,)),
-("mm", (5, 3, 0, 0,)),
-("qa", (6, 1,)),
-("mm", (5, 4, 0, 0,)),
-("qa", (7, 0,)),
-("mm", (5, 5, 0, 0,)),
-("mm", (6, 0, 0, 0,)),
-("qa", (7, 1,)),
-("mm", (6, 1, 0, 0,)),
-("mv", (0, 1, 64,)),
-("mm", (6, 2, 0, 0,)),
-("sc", (4, 0, 0, 1,)),
-("mm", (6, 3, 0, 0,)),
-("ms", (1, 1, 64,)),
-("mm", (7, 0, 0, 0,)),
-("qb", (0, 1,)),
-("st", (4, 0, 0, 1,)),
-("mm", (7, 1, 0, 0,)),
-("lb", (3, 1,)),
-("lb", (4, 1,)),
-("mm", (7, 2, 0, 0,)),
-("lb", (0, 2,)),
-("lb", (2, 2,)),
-("sc", (5, 0, 0, 1,)),
-("st", (3, 0, 0, 1,)),
-("mm", (7, 3, 0, 0,)),
-("mm", (6, 4, 0, 0,)),
-("mv", (1, 1, 64,)),
-("mm", (6, 5, 0, 0,)),
-("mv", (2, 1, 112,)),
-("mm", (4, 0, 1, 1,)),
-("ms", (2, 1, 112,)),
-("mm", (5, 0, 1, 1,)),
-("qb", (1, 1,)),
-("mm", (7, 4, 0, 0,)),
-("mm", (0, 0, 1, 0,)),
-("sc", (6, 0, 0, 1,)),
-("mm", (6, 0, 1, 1,)),
-("mm", (7, 5, 0, 0,)),
-("mm", (7, 0, 1, 1,)),
-("sc", (7, 0, 0, 1,)),
-("mm", (4, 1, 1, 1,)),
-("ms", (5, 1, 240,)),
-("mm", (1, 0, 1, 0,)),
-("qb", (2, 1,)),
-("mm", (6, 1, 1, 1,)),
-("st", (7, 0, 0, 1,)),
-("st", (2, 0, 0, 1,)),
-("lb", (3, 2,)),
-("mm", (0, 1, 1, 0,)),
-("st", (5, 0, 0, 1,)),
-("mm", (2, 0, 1, 0,)),
-("mv", (3, 1, 384,)),
-("mm", (5, 1, 1, 1,)),
-("ms", (3, 1, 384,)),
-("mm", (3, 0, 1, 0,)),
-("mm", (7, 1, 1, 1,)),
-("mm", (1, 1, 1, 0,)),
-("st", (6, 0, 0, 1,)),
-("mm", (1, 2, 1, 0,)),
-("mv", (4, 1, 80,)),
-("ms", (4, 1, 80,)),
-("mm", (7, 2, 1, 1,)),
-("qb", (3, 1,)),
-("mm", (6, 2, 1, 1,)),
-("mm", (3, 1, 1, 0,)),
-("mv", (5, 1, 240,)),
-("mm", (3, 2, 1, 0,)),
-("mm", (4, 2, 1, 1,)),
-("lb", (4, 2,)),
-("mv", (0, 2, 112,)),
-("mm", (2, 1, 1, 0,)),
-("mm", (0, 2, 1, 0,)),
-("ms", (0, 2, 112,)),
-("mm", (1, 3, 1, 0,)),
-("qb", (4, 1,)),
-("mm", (4, 3, 1, 1,)),
-("mm", (2, 2, 1, 0,)),
-("qb", (5, 1,)),
-("mm", (2, 3, 1, 0,)),
-("mm", (3, 3, 1, 0,)),
-("mv", (1, 2, 416,)),
-("mm", (7, 3, 1, 1,)),
-("mm", (0, 3, 1, 0,)),
-("ms", (1, 2, 416,)),
-("mm", (1, 4, 1, 0,)),
-("mm", (0, 4, 1, 0,)),
-("mv", (2, 2, 64,)),
-("ms", (2, 2, 64,)),
-("qb", (0, 2,)),
-("mm", (5, 2, 1, 1,)),
-("mm", (2, 4, 1, 0,)),
-("qb", (1, 2,)),
-("mm", (5, 3, 1, 1,)),
-("mm", (3, 4, 1, 0,)),
-("mm", (5, 4, 1, 1,)),
-("mm", (0, 5, 1, 0,)),
-("mm", (1, 5, 1, 0,)),
-("sc", (0, 1, 0, 1,)),
-("mm", (6, 3, 1, 1,)),
-("ms", (3, 2, 80,)),
-("mm", (5, 5, 1, 1,)),
-("sc", (1, 1, 0, 1,)),
-("mm", (6, 4, 1, 1,)),
-("st", (0, 1, 0, 1,)),
-("mm", (3, 5, 1, 0,)),
-("mv", (3, 2, 80,)),
-("mm", (2, 5, 1, 0,)),
-("st", (1, 1, 0, 1,)),
-("lb", (5, 2,)),
-("mm", (0, 0, 2, 0,)),
-("sc", (2, 1, 0, 1,)),
-("mm", (4, 4, 1, 1,)),
-("mm", (4, 5, 1, 1,)),
-("sc", (3, 1, 0, 1,)),
-("ms", (4, 2, 192,)),
-("mm", (1, 0, 2, 0,)),
-("mm", (7, 4, 1, 1,)),
-("qb", (2, 2,)),
-("mm", (0, 1, 2, 0,)),
-("mm", (2, 0, 2, 0,)),
-("sc", (4, 1, 0, 1,)),
-("mm", (7, 5, 1, 1,)),
-("mm", (2, 1, 2, 0,)),
-("sc", (5, 1, 0, 1,)),
-("mm", (1, 1, 2, 0,)),
-("mm", (3, 0, 2, 0,)),
-("mv", (4, 2, 192,)),
-("mm", (1, 2, 2, 0,)),
-("st", (5, 1, 0, 1,)),
-("st", (2, 1, 0, 1,)),
-("mm", (4, 0, 2, 1,)),
-("st", (3, 1, 0, 1,)),
-("st", (4, 1, 0, 1,)),
-("qb", (3, 2,)),
-("mm", (0, 2, 2, 0,)),
-("ms", (5, 2, 352,)),
-("mm", (2, 2, 2, 0,)),
-("qb", (4, 2,)),
-("mm", (6, 5, 1, 1,)),
-("mm", (3, 1, 2, 0,)),
-("mv", (5, 2, 352,)),
-("mm", (5, 0, 2, 1,)),
-("mm", (3, 2, 2, 0,)),
-("mm", (2, 3, 2, 0,)),
-("mm", (3, 3, 2, 0,)),
-("mm", (2, 4, 2, 0,)),
-("qb", (5, 2,)),
-("mm", (3, 4, 2, 0,)),
-("mm", (4, 1, 2, 1,)),
-("sc", (6, 1, 0, 1,)),
-("mm", (0, 3, 2, 0,)),
-("mm", (1, 3, 2, 0,)),
-("sc", (7, 1, 0, 1,)),
-("st", (6, 1, 0, 1,)),
-("mm", (4, 2, 2, 1,)),
-("mm", (0, 4, 2, 0,)),
-("st", (7, 1, 0, 1,)),
-("mm", (5, 1, 2, 1,)),
-("mm", (1, 4, 2, 0,)),
-("mm", (1, 5, 2, 0,)),
-("mm", (5, 2, 2, 1,)),
-("mm", (4, 3, 2, 1,)),
-("mm", (0, 5, 2, 0,)),
-("mm", (6, 0, 2, 1,)),
-("sc", (0, 2, 0, 1,)),
-("mm", (2, 5, 2, 0,)),
-("mm", (5, 3, 2, 1,)),
-("sc", (1, 2, 0, 1,)),
-("mm", (3, 5, 2, 0,)),
-("st", (0, 2, 0, 1,)),
-("mm", (6, 1, 2, 1,)),
-("sc", (2, 2, 0, 1,)),
-("mm", (7, 0, 2, 1,)),
-("st", (1, 2, 0, 1,)),
-("mm", (4, 4, 2, 1,)),
-("sc", (3, 2, 0, 1,)),
-("mm", (4, 5, 2, 1,)),
-("st", (2, 2, 0, 1,)),
-("mm", (6, 2, 2, 1,)),
-("sc", (4, 2, 0, 1,)),
-("mm", (5, 4, 2, 1,)),
-("st", (3, 2, 0, 1,)),
-("mm", (7, 1, 2, 1,)),
-("mm", (5, 5, 2, 1,)),
-("st", (4, 2, 0, 1,)),
-("mm", (6, 3, 2, 1,)),
-("sc", (5, 2, 0, 1,)),
-("mm", (6, 4, 2, 1,)),
-("mm", (6, 5, 2, 1,)),
-("mm", (7, 2, 2, 1,)),
-("st", (5, 2, 0, 1,)),
-("sc", (6, 2, 0, 1,)),
-("mm", (7, 3, 2, 1,)),
-("mm", (7, 4, 2, 1,)),
-("mm", (7, 5, 2, 1,)),
-("st", (6, 2, 0, 1,)),
-("sc", (7, 2, 1, 2,)),
-("sc", (7, 2, 0, 2,)),
-("st", (7, 2, 1, 2,)),
-("st", (7, 2, 0, 2,))])
+        def turn(m):
+            for q in range(3):
+                turn_a(m, q, tp_pool)
+            for q in range(3):
+                evac_a(m, q, nc.scalar.copy)
+
+        def quant(m):
+            quant_a(m, 0)
+            quant_a(m, 1)
+
+        def mix(g, n):
+            x = X[n] if isinstance(X[n], int) else X[n][g]
+            mix_b(g, n, x, True)
+            mix_b(g, n, x, False)
+
+        def bank(m, n):
+            return acc_pool if n == 0 or m < 4 else acc2_pool
+
+        def multiply_pass(ms, g, n):
+            for m in ms:
+                multiply(m, g, n, bank(m, n))
+
+        def multiply_tile(m, n):
+            for g in range(PASSES):
+                multiply(m, g, n, bank(m, n))
+
+        def finish(m, n, parts=1):
+            for h in range(parts):
+                scale(m, n, h, parts)
+
+        def put(m, n, parts=1):
+            for h in range(parts):
+                store(m, n, h, parts)
+
+        first = range(4)
         with tc.manual_schedule():
-            with tc.psum_pool(name="tp", bufs=TP) as tp_pool:
-                tp[0] = tp_pool
-                for name, a in part1:
-                    run(name, a)
-            acc2_pool = ctx.enter_context(tc.psum_pool(name="acc2", bufs=TP))
-            for name, a in part2:
-                run(name, a)
+            for kind in "A0 A1 A2 A3 B00 B01 B02 B03 B04 A4 B05 A5 A6 A7 B10 B11 B12 B13 B14 B15 B20 B21 B22 B23 B24 B25".split():
+                if kind[0] == "A":
+                    m = int(kind[1])
+                    load_a(m, 2 if m == 0 else 1)
+                else:
+                    load_b(int(kind[2]), int(kind[1]))
+            with tc.psum_pool(name="tp", bufs=4) as tp_pool:
+                permute(0)
+                for m in first:
+                    turn(m)
+                    if m < 3:
+                        permute(m + 1)
+                    else:
+                        mix(0, 0)
+                    quant(m)
+                for q in range(3):
+                    spread_pop(q, tp_pool)
+                quant_b(0, 0)
+                multiply_pass(first, 0, 0)
+                mix(1, 0)
+                mix(2, 0)
+                quant_b(1, 0)
+                multiply_pass(first, 1, 0)
+                mix(3, 0)
+                quant_b(2, 0)
+                multiply_pass(first, 2, 0)
+                for q in range(3):
+                    gather_pop(q)
+                quant_b(3, 0)
+                permute(4)
+                multiply_pass(first, 3, 0)
+                mix(4, 0)
+                mix(5, 0)
+                quant_b(4, 0)
+                turn(4)
+                permute(5)
+                multiply_pass(first, 4, 0)
+                quant_b(5, 0)
+                turn(5)
+                quant(4)
+                permute(6)
+                multiply_pass(first, 5, 0)
+                turn(6)
+                finish(0, 0)
+                quant(5)
+                finish(1, 0)
+                permute(7)
+                multiply_tile(4, 0)
+                mix(0, 1)
+                turn(7)
+                quant(6)
+                finish(2, 0)
+                finish(3, 0)
+                finish(4, 0)
+                quant(7)
+                mix(1, 1)
+                multiply_tile(5, 0)
+                quant_b(0, 1)
+                finish(5, 0)
+                multiply_tile(6, 0)
+                finish(6, 0)
+                mix(2, 1)
+                quant_b(1, 1)
+                multiply_tile(7, 0)
+                finish(7, 0)
+                for m in range(M_TILES):
+                    put(m, 0)
+            acc2_pool = ctx.enter_context(tc.psum_pool(name="acc2", bufs=4))
+            units = [(g, n) for n in (1, 2) for g in range(PASSES)]
+            mixed = [3]
+            quanted = [2]
+
+            def prepare(k):
+                for i in range(k):
+                    if mixed[0] < len(units):
+                        mix(*units[mixed[0]])
+                        mixed[0] += 1
+                    if quanted[0] < len(units):
+                        quant_b(*units[quanted[0]])
+                        quanted[0] += 1
+
+            last = (4, 5, 6, 7, 0, 1, 2, 3)
+            for g in range(4):
+                prepare(2)
+                multiply_pass(last, g, 1)
+            for m in last:
+                for g in (4, 5):
+                    multiply(m, g, 1, bank(m, 1))
+                finish(m, 1)
+                put(m, 1)
+                if m in (7, 1):
+                    prepare(1)
+            for g in range(PASSES):
+                multiply_pass((4, 5, 6, 7), g, 2)
+            for m in last:
+                if m < 4:
+                    multiply_tile(m, 2)
+                finish(m, 2, 2 if m == 3 else 1)
+                put(m, 2, 2 if m == 3 else 1)

@@ -184,7 +184,7 @@ def tile_rp3beta_item_walk_s2_kernel(tc, iu, ui, iv, vi, pop, out):
             )
 
 
-        X = {0: (400, 208, 208, 144, 144, 208), 1: 208, 2: 240}
+        X = {0: (400, 192, 192, 144, 144, 192), 1: 160, 2: 192}
 
         def permute(m):
             if m in range(8):

from contextlib import ExitStack

import concourse.mybir as mybir
from concourse.masks import make_identity

F32 = mybir.dt.float32
BF16 = mybir.dt.bfloat16
U32 = mybir.dt.uint32
U8 = mybir.dt.uint8
E4M3X4 = mybir.dt.float8_e4m3fn_x4
E5M2X4 = mybir.dt.float8_e5m2_x4

M, U, V, N = 1024, 2048, 1024, 1536
FLOPS = 2 * M * N * (U + V)
P = 128
K_PASS = 512
U_PASSES = U // K_PASS
V_PASSES = V // K_PASS
PASSES = U_PASSES + V_PASSES
M_TILES = M // P
N_TILE = 512
N_TILES = N // N_TILE
BETA = 0.6
POP_COLS = N // P


def tile_rp3beta_item_walk_s2_kernel(tc, iu, ui, iv, vi, pop, out):
    nc = tc.nc
    with ExitStack() as ctx:
        const = ctx.enter_context(tc.tile_pool(name="const", bufs=1))
        araw_pool = ctx.enter_context(tc.tile_pool(name="araw", bufs=6))
        agrp_pool = ctx.enter_context(tc.tile_pool(name="agrp", bufs=3))
        aperm_pool = ctx.enter_context(tc.tile_pool(name="aperm", bufs=4))
        codes_pool = ctx.enter_context(tc.tile_pool(name="codes", bufs=1))
        braw_pool = ctx.enter_context(tc.tile_pool(name="braw", bufs=13))
        bgrp_pool = ctx.enter_context(tc.tile_pool(name="bgrp", bufs=4))
        res_pool = ctx.enter_context(tc.tile_pool(name="res", bufs=8))
        acc_pool = ctx.enter_context(tc.psum_pool(name="acc", bufs=4))

        pop_sb = const.tile([P, POP_COLS], BF16, name="pop_sb")
        nc.scalar.dma_start(out=pop_sb[:], in_=pop.rearrange("(p c) -> p c", c=POP_COLS))
        ident = const.tile([P, P], F32, name="ident")
        make_identity(nc, ident[:])
        power = const.tile([P, POP_COLS], F32, name="power")
        nc.gpsimd.memset(power[:], 1.0)
        nc.gpsimd.tensor_scalar(power[:], power[:], -BETA, None, op0=mybir.AluOpType.mult)
        w_col = const.tile([P, POP_COLS], F32, name="w_col")
        nc.gpsimd.tensor_tensor(w_col[:], pop_sb[:], power[:], op=mybir.AluOpType.pow)
        w_row = const.tile([P, N], F32, name="w_row")

        a_raw = {}
        b_raw = {}
        a_codes = {}
        a_perm = {}
        accs = {}
        res = {}
        a_grp = {}
        b_grp = {}
        banks = {}
        a_scales = {}
        b_codes = {}
        b_scales = {}

        def load_a(m, pieces):
            raw = araw_pool.tile([P, U + V], BF16, name="a_raw")
            rows = slice(m * P, (m + 1) * P)
            step = U // pieces
            for c in range(0, U, step):
                nc.sync.dma_start(out=raw[:, c : c + step], in_=iu[rows, c : c + step])
            nc.sync.dma_start(out=raw[:, U:], in_=iv[rows, :])
            a_raw[m] = raw

        def load_b(g, n):
            raw = braw_pool.tile([P, 4, N_TILE], BF16, name="b_raw")
            src, row = (ui, g) if g < U_PASSES else (vi, g - U_PASSES)
            cols = slice(n * N_TILE, (n + 1) * N_TILE)
            nc.sync.dma_start(
                out=raw[:],
                in_=src[row * K_PASS : (row + 1) * K_PASS, cols].rearrange("(p j) w -> p j w", j=4),
            )
            b_raw[g, n] = raw

        def permute_a(m, q):
            words = a_raw[m][:, 1024 * q : 1024 * (q + 1)].bitcast(F32)
            a_perm[m, q] = aperm_pool.tile([P, 2, 2, P], F32, name="a_perm", align_bytes=64)
            nc.vector.tensor_copy(out=a_perm[m, q][:], in_=words.rearrange("p (g w u) -> p g u w", u=2, w=P))

        w_view = w_row[:].rearrange("p (n c) -> p n c", c=POP_COLS)

        def spread_pop(q, pool):
            banks["w", q] = pool.tile([P, 4, P], F32, name="tp")
            for c in range(4):
                col = 4 * q + c
                nc.tensor.transpose(banks["w", q][:, c, :], w_col[:, col : col + 1].to_broadcast([P, P]), ident[:])

        def gather_pop(q):
            nc.vector.tensor_copy(out=w_view[:, :, 4 * q : 4 * q + 4], in_=banks["w", q][:].rearrange("p c n -> p n c"))

        def turn_a(m, q, pool):
            bank = pool.tile([P, 2, 2, P], F32, name="tp")
            words = a_raw[m][:].bitcast(F32)
            for h in range(2):
                g = 2 * q + h
                for u in range(2):
                    if (m, q) in a_perm:
                        piece = a_perm[m, q][:, h, u, :]
                    else:
                        piece = words[:, 256 * g + u : 256 * (g + 1) : 2]
                    nc.tensor.transpose(bank[:, h, u, :], piece, ident[:])
            banks[m, q] = bank

        def evac_a(m, q, engine_copy):
            if m not in a_grp:
                a_grp[m] = agrp_pool.tile([P, PASSES, P, 4], BF16, name="a_grp", align_bytes=64)
            engine_copy(
                out=a_grp[m][:, 2 * q : 2 * q + 2].rearrange("p g r t -> p g (r t)").bitcast(F32).rearrange("p g (r u) -> p g r u", u=2),
                in_=banks[m, q][:].rearrange("p g u r -> p g r u"),
            )

        def quant_a(m, part):
            if m not in a_codes:
                a_codes[m] = codes_pool.tile([P, PASSES * P], U32, name="a_codes%d" % m, align_bytes=256)
                a_scales[m] = codes_pool.tile([P, PASSES * P], U8, name="a_scales%d" % m, align_bytes=256)
            flat = a_grp[m][:].rearrange("p g r t -> p (g r t)")
            split = U_PASSES * P
            cols = slice(0, split) if part == 0 else slice(split, PASSES * P)
            fmt = E4M3X4 if part == 0 else E5M2X4
            nc.vector.quantize_mx(
                out=a_codes[m][:, cols].bitcast(fmt),
                scales=a_scales[m][:, cols],
                in_=flat[:, 4 * cols.start : 4 * cols.stop],
            )

        def mix_b(g, n, x, on_vector):
            if (g, n) not in b_grp:
                b_grp[g, n] = bgrp_pool.tile([P, N_TILE, 4], BF16, name="b_grp", align_bytes=64)
            src = b_raw[g, n][:].rearrange("p t (c i) -> p c t i", i=4)
            dst = b_grp[g, n][:].rearrange("p (c i) t -> p c t i", i=4)
            if on_vector:
                nc.vector.tensor_copy(out=dst[:, : x // 4], in_=src[:, : x // 4])
            else:
                nc.scalar.copy(out=dst[:, x // 4 :], in_=src[:, x // 4 :])

        def quant_b(g, n):
            b_codes[g, n] = codes_pool.tile([P, N_TILE], U32, name="b_codes%d_%d" % (g, n), align_bytes=256)
            b_scales[g, n] = codes_pool.tile([P, N_TILE], U8, name="b_scales%d_%d" % (g, n), align_bytes=256)
            nc.vector.quantize_mx(
                out=b_codes[g, n][:].bitcast(E4M3X4),
                scales=b_scales[g, n][:],
                in_=b_grp[g, n][:].rearrange("p w t -> p (w t)"),
            )

        def multiply(m, g, n, pool):
            if g == 0:
                accs[m, n] = pool.tile([P, N_TILE], F32, name="acc")
            fmt = E4M3X4 if g < U_PASSES else E5M2X4
            cols = slice(g * P, (g + 1) * P)
            nc.tensor.matmul_mx(
                out=accs[m, n][:],
                lhsT=a_codes[m][:, cols].bitcast(fmt),
                lhsT_scale=a_scales[m][:, cols],
                rhs=b_codes[g, n][:].bitcast(E4M3X4),
                rhs_scale=b_scales[g, n][:],
                start=(g == 0),
                stop=(g == PASSES - 1),
            )

        def scale(m, n, h, parts):
            if (m, n) not in res:
                res[m, n] = res_pool.tile([P, N_TILE], F32, name="res_tile")
            w = N_TILE // parts
            nc.vector.tensor_tensor(
                res[m, n][:, h * w : (h + 1) * w],
                accs[m, n][:, h * w : (h + 1) * w],
                w_row[:, n * N_TILE + h * w : n * N_TILE + (h + 1) * w],
                op=mybir.AluOpType.mult,
            )

        def store(m, n, h, parts):
            w = N_TILE // parts
            nc.sync.dma_start(
                out=out[m * P : (m + 1) * P, n * N_TILE + h * w : n * N_TILE + (h + 1) * w],
                in_=res[m, n][:, h * w : (h + 1) * w],
            )


        X = {0: (400, 192, 192, 144, 144, 192), 1: 160, 2: 192}

        def permute(m):
            if m in range(8):
                for q in range(3):
                    permute_a(m, q)

        def turn(m):
            for q in range(3):
                turn_a(m, q, tp_pool)
            for q in range(3):
                evac_a(m, q, nc.scalar.copy)

        def quant(m):
            quant_a(m, 0)
            quant_a(m, 1)

        def mix(g, n):
            x = X[n] if isinstance(X[n], int) else X[n][g]
            mix_b(g, n, x, True)
            mix_b(g, n, x, False)

        def bank(m, n):
            return acc_pool if n == 0 or m < 4 else acc2_pool

        def multiply_pass(ms, g, n):
            for m in ms:
                multiply(m, g, n, bank(m, n))

        def multiply_tile(m, n):
            for g in range(PASSES):
                multiply(m, g, n, bank(m, n))

        def finish(m, n, parts=1):
            for h in range(parts):
                scale(m, n, h, parts)

        def put(m, n, parts=1):
            for h in range(parts):
                store(m, n, h, parts)

        first = range(4)
        with tc.manual_schedule():
            for kind in "A0 A1 A2 A3 B00 B01 B02 B03 B04 A4 B05 A5 A6 A7 B10 B11 B12 B13 B14 B15 B20 B21 B22 B23 B24 B25".split():
                if kind[0] == "A":
                    m = int(kind[1])
                    load_a(m, 2 if m == 0 else 1)
                else:
                    load_b(int(kind[2]), int(kind[1]))
            with tc.psum_pool(name="tp", bufs=4) as tp_pool:
                permute(0)
                for m in first:
                    turn(m)
                    if m < 3:
                        permute(m + 1)
                    else:
                        mix(0, 0)
                    quant(m)
                for q in range(3):
                    spread_pop(q, tp_pool)
                quant_b(0, 0)
                multiply_pass(first, 0, 0)
                mix(1, 0)
                mix(2, 0)
                quant_b(1, 0)
                multiply_pass(first, 1, 0)
                mix(3, 0)
                quant_b(2, 0)
                multiply_pass(first, 2, 0)
                for q in range(3):
                    gather_pop(q)
                quant_b(3, 0)
                permute(4)
                multiply_pass(first, 3, 0)
                mix(4, 0)
                mix(5, 0)
                quant_b(4, 0)
                turn(4)
                permute(5)
                multiply_pass(first, 4, 0)
                quant_b(5, 0)
                turn(5)
                quant(4)
                permute(6)
                multiply_pass(first, 5, 0)
                turn(6)
                finish(0, 0)
                quant(5)
                finish(1, 0)
                permute(7)
                multiply_tile(4, 0)
                mix(0, 1)
                turn(7)
                quant(6)
                finish(2, 0)
                finish(3, 0)
                finish(4, 0)
                quant(7)
                mix(1, 1)
                multiply_tile(5, 0)
                quant_b(0, 1)
                finish(5, 0)
                multiply_tile(6, 0)
                finish(6, 0)
                mix(2, 1)
                quant_b(1, 1)
                multiply_tile(7, 0)
                finish(7, 0)
                for m in range(M_TILES):
                    put(m, 0)
            acc2_pool = ctx.enter_context(tc.psum_pool(name="acc2", bufs=4))
            units = [(g, n) for n in (1, 2) for g in range(PASSES)]
            mixed = [3]
            quanted = [2]

            def prepare(k):
                for i in range(k):
                    if mixed[0] < len(units):
                        mix(*units[mixed[0]])
                        mixed[0] += 1
                    if quanted[0] < len(units):
                        quant_b(*units[quanted[0]])
                        quanted[0] += 1

            last = (4, 5, 6, 7, 0, 1, 2, 3)
            for g in range(4):
                prepare(2)
                multiply_pass(last, g, 1)
            for m in last:
                for g in (4, 5):
                    multiply(m, g, 1, bank(m, 1))
                finish(m, 1)
                put(m, 1)
                if m in (7, 1):
                    prepare(1)
            for g in range(PASSES):
                multiply_pass((4, 5, 6, 7), g, 2)
            for m in last:
                if m < 4:
                    multiply_tile(m, 2)
                finish(m, 2, 2 if m == 3 else 1)
                put(m, 2, 2 if m == 3 else 1)
